import numpy as np, ml_dtypes
CORES = [40,41,42,43,44,45,46,47]
N = 8
BF = ml_dtypes.bfloat16
def gentries(a):
    return np.ascontiguousarray(a.reshape(8, 16, -1).transpose(0, 2, 1)).reshape(8, -1)
def gtable(e):
    e = np.asarray(e); return np.ascontiguousarray(e.reshape(8, -1, 16).transpose(0, 2, 1)).reshape(128, -1).astype(np.int32)
W, UM, O, T, ST = 8192, 2048, 128, 4, 3
def parts(rng):
    x = rng.integers(0, 256, (N, 128, W), dtype=np.int16)
    p = rng.integers(0, W, (N, 8, W)); v = rng.integers(0, W, (N, 8, O, 16)); y = rng.integers(0, 256, (N, 128, O)); w = rng.integers(0, 256, (N, 128, 1))
    lm = np.zeros((N, 8, 2), np.int64)
    for q in range(N):
        lm[q, :, 0] = rng.permutation(np.array([400, 1000, 1150, 1300, 1400, 1550, 1700, 2600])) + rng.integers(-50, 51, 8)
        lm[q, :, 1] = rng.permutation(np.array([1100, 1200, 1300, 1400, 1500, 1600, 1700, 1800])) + rng.integers(-50, 51, 8)
    return x, p, v, y, w, lm
def pack(x, p, v, y, w, lm):
    return {"claim": np.ascontiguousarray(x).astype(np.float32).astype(BF), "par": np.ascontiguousarray(p).astype(np.int32), "who": np.stack([gtable(a.reshape(8, -1)) for a in v]),
            "est": np.ascontiguousarray(y).astype(np.float32).astype(BF), "wt": np.ascontiguousarray(w).astype(np.int32), "lim": np.ascontiguousarray(lm).astype(np.int32)}
def setup_inputs(rng):
    return pack(*parts(rng))
def setup_inputs_spread(rng):
    x, p, v, y, w, lm = parts(rng)
    x = (x.reshape(N, 8, 16, W) >> rng.integers(0, 9, (N, 8, 1, W)).astype(np.int16)).reshape(N, 128, W)
    p = np.minimum((W * rng.random(p.shape) ** 2).astype(np.int64), W - 1); v = np.minimum((W * rng.random(v.shape) ** 3).astype(np.int64), W - 1)
    y = (y.reshape(N, 8, 16, O) >> rng.integers(0, 9, (N, 8, 1, O))).reshape(N, 128, O); w = w >> rng.integers(0, 8, w.shape)
    lm = np.minimum(np.exp2(5 + 7 * rng.random(lm.shape)).astype(np.int64), 4080)
    return pack(x, p, v, y, w, lm)
def setup_inputs_ends(rng):
    c = rng.integers(0, 4, (N, 8, 1, W), dtype=np.int16); x = (255 * np.where(c < 2, c, rng.integers(0, 2, (N, 8, 16, W), dtype=np.int16))).reshape(N, 128, W)
    p = (W - 1) * rng.integers(0, 2, (N, 8, W))
    v = np.where(rng.random((N, 8, O, 1)) < 0.2, rng.integers(0, W, (N, 8, O, 16)), (W - 1) * rng.integers(0, 2, (N, 8, O, 16)))
    c = rng.integers(0, 4, (N, 8, 1, O)); y = (255 * np.where(c < 2, c, rng.integers(0, 2, (N, 8, 16, O)))).reshape(N, 128, O)
    w = 255 * rng.integers(0, 2, (N, 8, 16)); w[:, 3] = 0; w[:, 7] = 255; w = w.reshape(N, 128, 1)
    lm = np.full((N, 8, 2), 4080, np.int64)
    for q in range(N):
        for b in range(2): lm[q, :7, b] = 4080 * rng.permutation(np.array([0, 0, 0, 0, 1, 1, 1]))
    u = (16 * 255 * 255) & (UM - 1); hl = ((((W - 1) * u) >> 5) + W - 1) & (W - 1); h1 = ((u >> 5) + 1) & (W - 1)
    x[:, 112:, 0] = 0; x[:, 112:, hl] = 255; x[:, 112:, h1] = 255
    p[:, 7, 0] = W - 1; p[:, 7, 1] = 0; p[:, 7, W - 1] = 0
    y[:, 112:, O - 1] = 255; y[:, 112:, 3] = 255
    v[:, 7, O - 1] = 0; v[:, 7, O - 1, 14] = W - 1; v[:, 7, O - 1, 15] = 1
    v[:, 7, 3] = 0; v[:, 7, 3, 1] = W - 1; v[:, 7, 3, 2] = W - 1
    return pack(x, p, v, y, w, lm)
def setup_inputs_corners(rng):
    x, p, v, y, w, lm = parts(rng); sh = int(rng.integers(0, 8)); a = np.arange(W)
    for q in range(N):
        for g in range(8):
            m = (g + q + sh) % 8; lo, hi = 16 * g, 16 * g + 16
            if m == 0:
                p[q, g] = np.minimum(a + 1, W - 1); lm[q, g] = (4080, 1500); v[q, g, 0] = W - 1; v[q, g, 1] = 0; v[q, g, O - 1, 15] = W - 2
            elif m == 1:
                p[q, g] = a; lm[q, g] = (1, 0)
            elif m == 2:
                p[q, g] = 0; lm[q, g] = (0, 0); v[q, g] = rng.integers(0, W, (O, 1)); v[q, g, ::2] = W - 1
            elif m == 3:
                pool = np.concatenate([np.array([0, W - 1]), 1 + rng.permutation(W - 2)[:6]]); v[q, g] = pool[rng.integers(0, 8, (O, 16))]; p[q, g] = W - 1; lm[q, g] = (1300, 0)
            elif m == 4:
                w[q, lo:hi] = 0; lm[q, g] = (1, 0)
                e = rng.permutation(W)[:19]; c = x[q, lo:hi]
                c[:, e[:16]] = 255; c[np.arange(14), e[1:15]] = 0; c[14:, e[15]] = 0
                c[:, e[16:18]] = 0; c[:, e[18]] = 127
                p[q, g, e[:16]] = e[16]; p[q, g, e[16:18]] = e[1]; p[q, g, e[18]] = e[18]
                v[q, g, O - 1] = e[:16]
                v[q, g, O - 2] = e[:16]; v[q, g, O - 2, 0] = e[18]
                v[q, g, 0] = e[16]; v[q, g, 0, 0] = e[0]; v[q, g, O - 3] = e[17]; v[q, g, O - 3, 0] = e[0]
            elif m == 5:
                w[q, lo:hi] = 255; y[q, lo:hi] = 255; lm[q, g] = (1300, 4080)
            elif m == 6:
                v[q, g] = rng.permutation(W)[:16 * O].reshape(O, 16); lm[q, g] = (1200, 0)
            else:
                p[q, g] = W - 1 - a; w[q, lo:hi] = 0; w[q, lo + int(rng.integers(0, 16))] = 1; y[q, lo:hi, 0] = 0; lm[q, g] = (4080, 0)
    return pack(x, p, v, y, w, lm)
def setup_inputs_counts(rng):
    x, p, v, y, w, lm = parts(rng); a = int(rng.integers(0, N)); b = (a - ST) % N; d = (a - 2 * ST) % N; s = np.arange(W)
    p[d, :, :64] = np.arange(64); v[d] = rng.integers(0, 63, (8, O, 16)); lm[d, :, 0] = 1360 + rng.integers(-50, 51, 8)
    lm[b, :, 0] = 0; v[b] = rng.integers(64, W, (8, O, 16))
    w[a] = 0; x[a] = (x[a] & 63) + 191 * (s & 1)
    p[a] = (p[a] - (p[a] & 1)) + ((s + (s >= 64)) & 1); p[a, :, 63] = 63
    lm[a, :, 0] = 340 + rng.integers(-20, 21, 8); lm[a, :, 1] = 4080
    v[a] = rng.integers(64, W, (8, O, 16)); v[a, 7, O - 1] = 63; v[a, 0, 0, :15] = 63
    return pack(x, p, v, y, w, lm)
def setup_inputs_ties(rng):
    x, p, v, y, w, lm = parts(rng)
    z = np.stack([rng.permutation(np.array([1, 1, 3, 3, 8, 31, 64, 85])) for q in range(N)])
    x = ((x & 3).reshape(N, 8, 16, W) * z[:, :, None, None]).reshape(N, 128, W)
    lm = np.stack([z * rng.integers(17, 23, (N, 8)), z * rng.integers(18, 27, (N, 8))], axis=2)
    v[:, ::3] = v[:, ::3] & 63
    return pack(x, p, v, y, w, lm)
def check_inputs(d):
    bad = []
    for k, lo, hi in (("claim", 0, 255), ("par", 0, W - 1), ("who", 0, W - 1), ("est", 0, 255), ("wt", 0, 255), ("lim", 0, 4080)):
        a = np.asarray(d[k]).astype(np.float32)
        if not (np.min(a) >= lo and np.max(a) <= hi): bad.append("range of " + k)
        elif not np.all(np.floor(a) == a): bad.append("whole numbers of " + k)
    return bad
def place(s, u, t):
    return (((s * u[:, :, None]) >> 5) + s + 77 * t) & (W - 1)
def reference(claim, par, who, est, wt, lim):
    X = np.ascontiguousarray(np.asarray(claim).astype(np.float32).astype(np.int32).reshape(N, 8, 16, W).transpose(0, 1, 3, 2))
    P = np.asarray(par).astype(np.int64); V = np.stack([gentries(a) for a in who]).astype(np.int64).reshape(N, 8, O, 16)
    Y = np.ascontiguousarray(np.asarray(est).astype(np.float32).astype(np.int64).reshape(N, 8, 16, O).transpose(0, 1, 3, 2))
    wq = np.asarray(wt).astype(np.int64).reshape(N, 8, 1, 16); lm = np.asarray(lim).astype(np.int64)
    G = np.arange(8)[:, None]; cnt = [0] * N
    for t in range(T):
        for q in range(N):
            r = (q - ST * t) % N; v = V[r]; y0 = Y[r]
            u = np.add.reduce(wq[q] * y0, axis=2) & (UM - 1)
            p = P[q][G, v.reshape(8, -1)].reshape(8, O, 16)
            x = X[q][G, place(v, u, t).reshape(8, -1)].reshape(8, O, 16, 16)
            z = X[q][G, place(p, u, t).reshape(8, -1)].reshape(8, O, 16, 16)
            dep = np.add.reduce(np.abs(x - z), axis=3) < lm[q, :, 0][:, None, None] + cnt[q]
            cand = ~dep | np.all(dep, axis=2, keepdims=True)
            M = (np.max(np.where(cand[..., None], x, -1), axis=2) + np.min(np.where(cand[..., None], x, 256), axis=2)) >> 1
            far = np.where(cand, np.add.reduce(np.abs(x - M[:, :, None, :]), axis=3), 1 << 20)
            y = np.take_along_axis(x, np.argmin(far, axis=2)[:, :, None, None], 2)[:, :, 0, :]
            err = np.add.reduce(np.abs(x - y[:, :, None, :]), axis=3)
            j = np.argmax(err, axis=2)[:, :, None]; rest = np.where(np.arange(16) == j, -1, err); k = np.argmax(rest, axis=2)[:, :, None]
            ask = np.take_along_axis(rest, k, 2)[:, :, 0] >= lm[q, :, 1][:, None]
            vj = np.take_along_axis(v, j, 2)[:, :, 0]; vk = np.take_along_axis(v, k, 2)[:, :, 0]
            for g in range(8):
                o = np.nonzero(ask[g])[0]
                if len(o):
                    s, first = np.unique(vk[g, o], return_index=True)
                    P[q, g, s] = vj[g, o[first]]
            V[r] = np.where(dep, p, v); Y[r] = (y0 + y) >> 1
            cnt[q] = int(np.count_nonzero(dep)) & 31
    return {"yv": np.stack([gtable(a.reshape(8, -1)) for a in V]).astype(np.float32), "ye": np.ascontiguousarray(Y.transpose(0, 1, 3, 2)).reshape(N, 128, O).astype(np.float32).astype(BF), "yp": P.astype(np.float32)}

@@ -1,0 +1,499 @@
+from concourse.mybir import AluOpType as O, AxisListType, ActivationFunctionType as F
+
+SCRATCH = {}
+SEMAPHORES = ["qv", "qs", "qt", "qg", "ls"]
+BF, F4, H2, I4, U2 = "bfloat16", "float32", "float16", "int32", "uint16"
+
+
+def _b(name, cols, dtype="float32", where="sbuf"):
+    SCRATCH[name] = (where, [128, cols], dtype)
+
+
+for _n, _c, _d in [
+        ("CL", 8192, BF), ("TB", 8320, BF), ("T32", 8320, F4),
+        ("X0", 2048, BF), ("X1", 2048, BF), ("XS0", 2064, H2), ("XS1", 2064, H2),
+        ("PG", 2048, BF), ("DZ", 2048, BF), ("AD", 2048, BF), ("SG", 2048, BF),
+        ("SA", 2048, F4), ("SB", 2048, F4), ("FD", 2048, BF), ("FA", 2048, BF), ("ED", 2048, BF), ("EA", 2048, BF),
+        ("VF0", 128, F4), ("VF1", 128, F4), ("S32", 128, F4), ("UI", 128, I4), ("UQ0", 128, I4), ("UQ1", 128, I4), ("HA", 128, F4), ("HB", 128, I4), ("HC", 128, I4), ("HX", 128, U2),
+        ("S3P", 128, F4), ("PA", 128, F4), ("PB", 128, I4), ("PC", 128, I4), ("HZ", 128, U2),
+        ("PV", 128, F4), ("DP", 128, F4), ("VN", 128, F4), ("DM", 128, BF), ("VT", 144, F4),
+        ("SS", 128, F4), ("MH", 128, H2), ("QP", 136, F4), ("QY", 136, F4), ("YV", 128, BF), ("YS", 128, F4), ("YL", 8, U2),
+        ("MN", 128, F4), ("MM", 128, F4), ("MR", 128, F4), ("K2S", 144, F4), ("M1", 144, F4), ("M2", 144, F4), ("DD", 144, F4),
+        ("OB", 144, F4), ("OA", 144, F4), ("OBV", 144, F4), ("OAV", 144, F4), ("VB", 144, F4), ("VA", 144, F4),
+        ("ND", 144, F4), ("OFS", 144, F4), ("OFF", 128, F4), ("OFM", 128, F4), ("VAF", 128, F4), ("D32", 128, F4), ("DR", 128, F4), ("DW", 128, F4), ("DB", 128, BF),
+        ("L16", 8, U2), ("LC", 8, U2), ("L17", 9, U2), ("LI16", 8, F4), ("LIC", 9, F4), ("CI9", 9, F4), ("CG9", 9, F4), ("LS9", 9, F4), ("IDW", 144, F4),
+        ("EQ", 1024, BF), ("ST", 1024, BF), ("LO", 8, F4), ("LO2", 8, F4), ("OFL", 8, F4), ("OFU", 8, U2),
+        ("CN", 1, F4), ("CI", 1, I4), ("CJ", 1, I4), ("THC", 1, F4), ("SBI", 1, F4), ("TH", 1, F4),
+        ("ONB", 512, BF), ("ONF", 256, F4), ("IDB", 128, BF), ("IDP", 128, BF), ("IDN", 128, BF), ("IDF", 128, F4),
+        ("BK0", 128, BF), ("BLK", 128, BF), ("BL8", 8, BF), ("SR", 8, BF), ("DK", 2048, BF), ("EK", 2048, BF), ("WB", 128, H2), ("WC1", 1, F4), ("WC2", 1, F4), ("WCE", 1, F4), ("C1", 1, F4),
+        ("PI4", 1, I4), ("PI5", 1, I4), ("PM", 1, F4), ("PM16", 1, F4), ("DCOL", 1, F4), ("THR", 1, F4), ("THB", 1, F4),
+        ("PEN", 128, BF), ("KI", 136, F4), ("KC", 128, BF), ("KN", 136, F4), ("KN2", 136, F4), ("K2T", 136, F4), ("K2R", 144, F4), ("IW", 136, F4),
+        ("JI", 128, F4), ("NK", 1, F4), ("NKH", 1, H2), ("MASKJ", 128, F4), ("RSEL", 8, F4), ("NRS", 8, F4), ("L0", 8, F4), ("LBASE", 8, F4), ("DU0", 8, F4), ("DUM", 8, F4),
+        ("RMX", 512, BF), ("RMN", 512, BF), ("KMN", 128, F4), ("KMX", 144, F4), ("GRO", 1024, BF), ("SEL8", 128, F4),
+        ("PAR", 512, I4), ("PF", 512, F4), ("P64", 512, F4), ("PH", 512, BF), ("PL", 512, BF),
+        ("WI", 128, I4), ("E0", 128, BF), ("WT", 1, I4), ("WF", 1, F4), ("CW", 1, F4), ("LI", 2, I4), ("LF", 2, F4), ("N16", 1, F4),
+        ("YVF", 128, F4), ("YEB", 128, BF)]:
+    _b(_n, _c, _d)
+for _t in range(5):
+    for _n, _d in (("VU", U2), ("YH", H2), ("VO", U2), ("YO", H2)):
+        _b("%s%d" % (_n, _t), 128, _d)
+    SEMAPHORES += ["rv%d" % _t, "ry%d" % _t]
+AL = {}
+_pos = {}
+for _n in list(SCRATCH):
+    _w, _s, _d = SCRATCH[_n]
+    if _s[1] <= 256 and _d in (BF, F4, I4):
+        _p = _pos.get(_d, 0)
+        AL[_n] = ("ALL_" + _d, _p, _s[1])
+        _pos[_d] = _p + (_s[1] + 15) // 16 * 16
+        del SCRATCH[_n]
+for _d in _pos:
+    _b("ALL_" + _d, _pos[_d], _d)
+PSUM = ("R0", "R1", "R2", "R3", "D0", "D1", "S0", "S1")
+for _n in PSUM:
+    _b(_n, 512, F4, "psum")
+SEMAPHORES += ["d%d" % i for i in range(20)]
+
+NS = 8
+CH = 4
+QX = "ssss"
+QP = "svsv"
+CUT = 2
+MAG16, MAG64 = 1.5 * 2.0 ** 27, 1.5 * 2.0 ** 29
+
+
+def rank_program(g, core, T, topo):
+    rank = T.rank_of(core)
+    if rank is None:
+        return
+    N = len(T.cores)
+    eng = {"v": g.vector, "s": g.scalar, "t": g.tensor, "g": g, "y": g.sync}
+    cnt = {"v": 0, "s": 0, "t": 0, "g": 0}
+    tot, snap, hist, ndma = {}, {}, {}, [0]
+    know = {q: {} for q in eng}
+
+    def need(q, ins, outs):
+        req = {}
+
+        def add(e):
+            if know[q].get(e[0], 0) < e[1]:
+                req[e[0]] = max(req.get(e[0], 0), e[1])
+        for (_, n, a, b) in ins:
+            for (wa, wb, k, wq, e) in hist.get(n, ()):
+                if n in PSUM:
+                    if wq != q:
+                        add(e)
+                elif wa < b and a < wb and k == "w":
+                    add(e)
+        for (_, n, a, b) in outs:
+            for (wa, wb, k, wq, e) in hist.get(n, ()):
+                if n in PSUM:
+                    if wq != q:
+                        add(e)
+                elif wa < b and a < wb and (wq != q or e[0][0] != "q" or k == "w"):
+                    add(e)
+        for s in list(req):
+            for s2 in list(req):
+                if s2 != s and s in req and s2 in req and snap[(s2, req[s2])].get(s, 0) >= req[s]:
+                    del req[s]
+        for s in sorted(req):
+            eng[q].wait_ge(T.sem[s], req[s])
+            for k2, v2 in snap[(s, req[s])].items():
+                know[q][k2] = max(know[q].get(k2, 0), v2)
+            know[q][s] = max(know[q].get(s, 0), req[s])
+
+    def note(q, ins, outs, e):
+        for (_, n, a, b) in outs:
+            h = hist.setdefault(n, [])
+            if n in PSUM:
+                h[:] = [x for x in h if x[3] == q and x[4][1] > e[1]]
+            else:
+                h[:] = [x for x in h if not (a <= x[0] and x[1] <= b)]
+            h.append((a, b, "w", q, e))
+        for (_, n, a, b) in ins:
+            h = hist.setdefault(n, [])
+            h[:] = [x for x in h if not (x[2] == "r" and x[3] == q and x[4][0] == e[0] and a <= x[0] and x[1] <= b)]
+            h.append((a, b, "r", q, e))
+
+    def op(q, fn, outs, ins):
+        need(q, ins, outs)
+        s = "q" + q
+        cnt[q] += 1
+        snap[(s, cnt[q])] = dict(know[q])
+        tot[s] = cnt[q]
+        fn(eng[q]).then_inc(T.sem[s], 1)
+        note(q, ins, outs, (s, cnt[q]))
+
+    def dma(q, out, in_):
+        need(q, [in_], [out])
+        s = "d%d" % ndma[0]
+        ndma[0] += 1
+        snap[(s, 16)] = dict(know[q])
+        tot[s] = 16
+        eng[q].dma_start(out[0], in_[0]).then_inc(T.sem[s], 16)
+        note(q, [in_], [out], (s, 16))
+
+    def r(n, a=0, b=None, st=1, p=None):
+        if n in AL:
+            n, o, w = AL[n]
+            b = min(o + (w if b is None else b), o + w)
+            a = o + a
+        b = T[n].shape[1] if b is None else b
+        return (T[n][0:p, a:b:st] if p else T[n][:, a:b:st], n, a, b)
+
+    def inp(ap, name):
+        return (ap, name, 0, 1)
+
+    def val(x):
+        return x[0] if isinstance(x, tuple) else x
+
+    def aps(*xs):
+        return [x for x in xs if isinstance(x, tuple)]
+
+    def tt(out, a, b, o):
+        op("v", lambda e: e.tensor_tensor(out=out[0], in0=a[0], in1=b[0], op=o), [out], [a, b])
+
+    def ts(out, a, s1, o1, s2=None, o2=None):
+        if o2 is None:
+            op("v", lambda e: e.tensor_scalar(out=out[0], in0=a[0], scalar1=val(s1), scalar2=None, op0=o1), [out], aps(a, s1))
+        else:
+            op("v", lambda e: e.tensor_scalar(out=out[0], in0=a[0], scalar1=val(s1), scalar2=val(s2), op0=o1, op1=o2), [out], aps(a, s1, s2))
+
+    def cp(out, a, q="v"):
+        if q == "v":
+            op("v", lambda e: e.tensor_copy(out=out[0], in_=a[0]), [out], [a])
+        else:
+            op("s", lambda e: e.activation(out=out[0], in_=a[0], func=F.Copy), [out], [a])
+
+    def act(out, a, f, bias=0.0, scale=1.0):
+        op("s", lambda e: e.activation(out=out[0], in_=a[0], func=f, bias=val(bias), scale=val(scale)), [out], aps(a, bias, scale))
+
+    def scan(out, d0, d1, init, o0, o1):
+        op("v", lambda e: e.tensor_tensor_scan(out=out[0], data0=d0[0], data1=d1[0], initial=val(init), op0=o0, op1=o1), [out], aps(d0, d1, init))
+
+    def ms(a, c):
+        op("v", lambda e: e.memset(a[0], c), [a], [])
+
+    def mm(out, l, rh, start, stop):
+        op("t", lambda e: e.matmul(out[0], lhsT=l[0], rhs=rh[0], start=start, stop=stop), [out], [l, rh])
+
+    def aff(out, a, pat, cmp, fill, base, chm):
+        op("g", lambda e: e.affine_select(out=out[0], in_=a[0], pattern=pat, compare_op=cmp, fill=fill, base=base, channel_multiplier=chm), [out], [a])
+
+    def iota(out, pat, base, chm):
+        op("g", lambda e: e.iota(out[0], pattern=pat, base=base, channel_multiplier=chm, allow_small_or_imprecise_dtypes=True), [out], [])
+
+    def gather(q, out, win, off, in1=None, o=None):
+        ap = win[0].indirect(off[0])
+        if in1 is not None:
+            op("v", lambda e: e.tensor_tensor(out=out[0], in0=ap, in1=in1[0], op=o), [out], [win, off, in1])
+        elif q == "v":
+            op("v", lambda e: e.tensor_copy(out=out[0], in_=ap), [out], [win, off])
+        else:
+            op("s", lambda e: e.activation(out=out[0], in_=ap, func=F.Copy), [out], [win, off])
+
+    def scatter(win, off, src):
+        ap = win[0].indirect(off[0])
+        op("v", lambda e: e.tensor_copy(out=ap, in_=src[0]), [win], [off, src])
+
+    def send(to, src, dst, sem):
+        c = T.cores[to % N]
+        need("g", [src], [])
+        m = sum(1 << e for e in topo.engines(core, c)[:NS])
+        rid, pid, _ = topo.addr(c)
+        g.remote_dma(out_ap=T[dst][:], in_ap=src[0], remote_sem=T.sem[sem], local_sem=T.sem.ls, pid=pid, routing_id=rid, dma_engine_mask=m)
+        tot["ls"] = tot.get("ls", 0) + NS
+
+    def landed(n, sem):
+        tot[sem] = NS
+        snap[(sem, NS)] = {}
+        hist[n] = [(0, 128, "w", "far", (sem, NS))]
+
+    def ck(n, c):
+        return r(n, 512 * c, 512 * c + 512)
+
+    def lk(n, c):
+        return r(n, 32 * c, 32 * c + 32)
+
+    def start():
+        dma("s", r("PAR"), inp(T.par[:], "par"))
+        dma("y", r("WI"), inp(T.who[:], "who"))
+        dma("s", r("E0"), inp(T.est[:], "est"))
+        dma("y", r("WT"), inp(T.wt[:], "wt"))
+        dma("s", r("LI", 0, 2, 1, 8), inp(T.lim[:], "lim"))
+        dma("y", r("CL"), inp(T.claim[:], "claim"))
+        ms(r("ONB"), 1.0)
+        ms(r("ONF"), 1.0)
+        iota(r("PI4"), [[0, 1]], 0, 1)
+        aff(r("BK0"), r("ONB", 0, 128), [[-16, 8], [0, 16]], O.is_ge, 0.0, 0, 1)
+        aff(r("BLK"), r("BK0"), [[16, 8], [0, 16]], O.is_ge, 0.0, 15, -1)
+        aff(r("SEL8", p=8), r("ONF", 0, 128, 1, 8), [[-1, 8], [0, 16]], O.is_equal, 0.0, 0, 1)
+        aff(r("IDB"), r("ONB", 0, 128), [[-1, 128]], O.is_equal, 0.0, 0, 1)
+        ms(r("NK"), -1024.0)
+        ms(r("DK"), 0.0)
+        ms(r("TB"), 0.0)
+        cp(r("PF"), r("PAR"))
+        ts(r("P64"), r("PF"), MAG64, O.add, MAG64, O.subtract)
+        ts(r("PH"), r("P64"), -1.0, O.mult)
+        tt(r("PL"), r("PF"), r("P64"), O.subtract)
+        dma("y", (T.TB[1:128:16, 0:8192], "TB", 0, 8192), r("PH"))
+        dma("s", (T.TB[2:128:16, 0:8192], "TB", 0, 8192), r("PL"))
+        dma("y", (T.T32[0:128:16, 0:8192], "T32", 0, 8192), r("PF"))
+        cp(r("VU0"), r("WI"))
+        cp(r("WF"), r("WT"))
+        ts(r("WB"), r("BLK"), r("WF"), O.mult)
+        ts(r("YH0"), r("E0"), 1024.0, O.add)
+        cp(r("NKH"), r("NK"))
+        mm(r("S0", 496, 497), r("WB"), r("NKH"), True, True)
+        cp(r("CW"), r("S0", 496, 497))
+        cp(r("BL8"), r("BLK", 0, 128, 16))
+        ts(r("PI5"), r("PI4"), 15, O.bitwise_and)
+        cp(r("PM"), r("PI5"))
+
+    def constants():
+        for k in range(16):
+            cp(r("DK", 128 * k + k, 128 * k + 128, 16), r("BL8"), "s")
+        ts(r("WC1"), r("PM"), 1.0, O.is_equal)
+        ts(r("WC2"), r("PM"), 2.0, O.is_equal)
+        tt(r("WCE"), r("WC2"), r("WC1"), O.subtract)
+        ts(r("EK"), r("DK"), r("WCE"), O.mult)
+        ts(r("C1"), r("PM"), 1.0, O.not_equal)
+        cp(r("LF", 0, 2, 1, 8), r("LI", 0, 2, 1, 8))
+        ts(r("N16", 0, 1, 1, 8), r("LF", 1, 2, 1, 8), -16.0, O.mult)
+        mm(r("S0", 498, 499), r("SEL8", 0, 128, 1, 8), r("LF", 0, 1, 1, 8), True, True)
+        cp(r("TH"), r("S0", 498, 499))
+        cp(r("THC"), r("TH"))
+        ts(r("SBI"), r("TH"), -1.0, O.mult, 0.5, O.add)
+        ts(r("IDP"), r("IDB"), 128.0, O.mult)
+        ts(r("IDN"), r("IDB"), -128.0, O.mult)
+        cp(r("IDF"), r("IDB"))
+        ts(r("SR"), r("BL8"), 16.0, O.mult)
+        cp(r("RSEL"), r("BL8"))
+        ts(r("NRS"), r("RSEL"), -1.0, O.mult)
+        ts(r("PM16"), r("PM"), 16.0, O.mult)
+        ms(r("IDW"), 0.0)
+        aff(r("IW"), r("ONF", 0, 136), [[-16, 8], [-1, 17]], O.is_equal, 0.0, 1, 1)
+        aff(r("IDW", 0, 136), r("IW"), [[0, 8], [1, 17]], O.is_gt, 0.0, 0, 0)
+        ms(r("RMX"), 1024.0)
+        ms(r("RMX", 0, 512, 16), -1024.0)
+        ms(r("RMN"), -1024.0)
+        ms(r("RMN", 0, 512, 16), 1024.0)
+        ms(r("QP", 0, 1), 0.0)
+        ms(r("QY", 0, 1), 0.0)
+        iota(r("JI"), [[0, 8], [1, 16]], 0, 0)
+        ts(r("KC"), r("JI"), -7.5, O.add)
+        ts(r("MASKJ"), r("JI"), r("PM"), O.is_equal)
+        ts(r("PEN"), r("IDB"), 65536.0, O.mult)
+        iota(r("LI16"), [[16, 8]], 15, 0)
+        cp(r("L16"), r("LI16"))
+        iota(r("LIC"), [[17, 9]], 16, 0)
+        cp(r("LC"), r("LIC", 0, 8))
+        iota(r("CI9"), [[1, 9]], 0, 0)
+        ts(r("CG9"), r("CI9"), r("PM"), O.is_gt, -17.0, O.mult)
+        tt(r("LS9"), r("LIC"), r("CG9"), O.add)
+        ts(r("L17"), r("LS9"), 143.0, O.min)
+        iota(r("L0"), [[256, 8]], 0, 0)
+        ts(r("LBASE"), r("L0"), r("PM16"), O.add, 7.5, O.add)
+        ms(r("KMN"), -8388608.0)
+        ms(r("KMN", 0, 128, 16), 8388608.0)
+        iota(r("KI"), [[0, 8], [1, 17]], 0, 0)
+        ts(r("KN"), r("KI"), -1.0, O.mult, 17.0, O.add)
+        aff(r("KN2"), r("KN"), [[0, 8], [1, 17]], O.is_gt, -4194304.0, 0, 0)
+        ts(r("K2T", 0, 136, 1, 8), r("KN2", 0, 136, 1, 8), r("N16", 0, 1, 1, 8), O.add)
+        ms(r("K2R"), 0.0)
+        aff(r("K2R", 0, 136, 1, 8), r("K2T", 0, 136, 1, 8), [[-1, 8], [0, 17]], O.is_equal, 0.0, 0, 1)
+        ms(r("KMX"), 8388608.0)
+        ms(r("KMX", 0, 144, 17), -8388608.0)
+        ms(r("DD"), -8388608.0)
+        iota(r("DCOL"), [[0, 1]], 8192, 1)
+        iota(r("DU0"), [[16, 8]], 8192, 0)
+        ts(r("DUM"), r("DU0"), r("PM"), O.add)
+        ms(r("GRO"), 1.5)
+        ms(r("GRO", 0, 1024, 128), 0.0)
+        ms(r("EQ"), 0.0)
+        ms(r("THB"), 6.3051201)
+        act(r("THR"), r("PM"), F.Exp, r("THB"), -0.4054651)
+
+    def names(t):
+        cp(r("VF%d" % (t & 1)), r("VU%d" % t))
+        act(r("S32"), r("VF%d" % (t & 1)), F.Copy, 32.0 * 77 * t - 262144.0, 32.0)
+
+    def hashes(t):
+        UQ = "UQ%d" % (t & 1)
+        mm(r("S0", 0, 128), r("WB"), r("YH%d" % t), True, True)
+        ts(r("UI"), r("S0", 0, 128), r("CW"), O.add)
+        ts(r(UQ), r("UI"), 2047, O.bitwise_and)
+        tt(r("HA"), r("VF%d" % (t & 1)), r(UQ), O.mult)
+        tt(r("HB"), r("HA"), r("S32"), O.add)
+        ts(r("HC"), r("HB"), 5, O.arith_shift_right, 8191, O.bitwise_and)
+        cp(r("HX"), r("HC"))
+
+    def claims(t):
+        for c in range(CH):
+            gather(QX[c], ck("X%d" % (t & 1), c), r("CL"), lk("HX", c))
+
+    def shifted(t):
+        for c in range(CH):
+            cp(r("XS%d" % (t & 1), 512 * c + 1, 512 * c + 513), ck("X%d" % (t & 1), c))
+
+    def main(t):
+        p = t & 1
+        X, XS, VF, UQ = "X%d" % p, "XS%d" % p, "VF%d" % p, "UQ%d" % p
+        R, R2 = ["R0", "R1", "R2", "R3"], ["D0", "D1", "R0", "R1"]
+        to = rank + (3 if t < 3 else -9)
+        for c in range(CH):
+            gather(QP[c], ck("PG", c), r("TB", 0, 8192), lk("VU%d" % t, c))
+
+        def masked(c):
+            mm(r(R[c]), r("IDP"), ck("SG", c), False, True)
+
+        def turned(c):
+            mm(r(R2[c]), r("IDB"), ck(X, c), True, False)
+            mm(r(R2[c]), r("IDN"), ck("SG", c), False, True)
+
+        for c in range(CH):
+            mm(r(R[c]), r("IDB"), ck(X, c), True, False)
+        for h in range(CUT):
+            w = 128 // CUT
+            a, b = w * h, w * h + w
+            for k in range(16):
+                mm(r("S0", 128 + a, 128 + b), r("EK", 128 * k, 128 * k + 128), r("PG", 16 * a + k, 16 * b, 16), k == 0, k == 15)
+            tt(r("PA", a, b), r("S0", 128 + a, 128 + b), r(UQ, a, b), O.mult)
+            act(r("S3P", a, b), r("S0", 128 + a, 128 + b), F.Copy, 32.0 * 77 * t - 262144.0, 32.0)
+            tt(r("PB", a, b), r("PA", a, b), r("S3P", a, b), O.add)
+            ts(r("PC", a, b), r("PB", a, b), 5, O.arith_shift_right, 8191, O.bitwise_and)
+            cp(r("HZ", a, b), r("PC", a, b))
+            for c in range(CH * h // CUT, CH * (h + 1) // CUT):
+                gather("v", ck("DZ", c), r("CL"), lk("HZ", c), ck(X, c), O.subtract)
+                act(ck("AD", c), ck("DZ", c), F.Abs)
+                mm(r("D%d" % (c & 1)), r("BLK"), ck("AD", c), True, True)
+                act(ck("SG", c), r("D%d" % (c & 1)), F.Sign, r("SBI"))
+                if c:
+                    masked(c - 1)
+        masked(CH - 1)
+        turned(0)
+        turned(1)
+        tt(r("PV"), r("S0", 128, 256), r(VF), O.subtract)
+        shifted(t)
+        for c in range(CH):
+            scan(ck("SA", c), r("RMX"), r(R[c]), 0.0, O.min, O.max)
+            if c < 2:
+                turned(c + 2)
+        for k in range(16):
+            mm(r("S1", 0, 128), r("DK", 128 * k, 128 * k + 128), r("AD", k, 2048, 16), k == 0, k == 15)
+        mm(r("S1", 128, 272), r(VF), r("IDW"), True, True)
+        for c in range(CH):
+            scan(ck("SB", c), r("RMN"), r(R2[c]), 0.0, O.max, O.min)
+        tt(r("SS"), r("SA", 15, 2048, 16), r("SB", 15, 2048, 16), O.add)
+        ts(r("MH"), r("SS"), 0.5, O.mult, 1023.8, O.add)
+        tt(r("QP", 1, 129), r("MH"), r(X, 15, 2048, 16), O.subtract)
+        tt(r(XS, 0, 2048, 16), r("MH"), r("QP", 0, 128), O.subtract)
+        for c in range(CH):
+            scan(ck("FD", c), ck(XS, c), ck(X, c), -1024.0 if c == 0 else r("FD", 512 * c - 1, 512 * c), O.add, O.subtract)
+            act(ck("FA", c), ck("FD", c), F.Abs)
+        ts(r("DM"), r("S1", 0, 128), r("THC"), O.is_lt)
+        cp(r("VT"), r("S1", 128, 272), "s")
+        mm(r("S1", 0, 128), r("ONB", 0, 128, 1, 1), r("KC", 0, 128, 1, 1), True, False)
+        mm(r("S1", 0, 128), r("DM"), r("PEN"), False, False)
+        for k in range(16):
+            mm(r("S1", k, 128, 16), r("FA", k, 2048, 16), r("SR"), False, k == 15)
+        mm(r("S0", 256, 264), r("IDF"), r("LBASE"), True, False)
+        tt(r("DP"), r("PV"), r("DM"), O.mult)
+        tt(r("VN"), r("DP"), r(VF), O.add)
+        cp(r("VO%d" % t), r("VN"))
+        send(to, r("VO%d" % t), "VU%d" % (t + 1), "rv%d" % (t + 1))
+        if t < 3:
+            count()
+        scan(r("MN"), r("KMN"), r("S1", 0, 128), 0.0, O.max, O.min)
+        gather("v", r("MM"), r("MN"), r("L16"), r("MASKJ"), O.mult)
+        mm(r("S0", 256, 264), r("MM"), r("RSEL"), False, False)
+        ts(r("MR"), r("MM"), MAG16, O.add, MAG16, O.subtract)
+        mm(r("S0", 256, 264), r("MR"), r("NRS"), False, True)
+        cp(r("YL"), r("S0", 256, 264))
+        gather("s", r("YV"), r(X), r("YL"))
+        gather("v", r("YS"), r(X), r("YL"), r("YH%d" % t), O.add)
+        ts(r("YO%d" % t), r("YS"), 0.5, O.mult, 511.8, O.add)
+        send(to, r("YO%d" % t), "YH%d" % (t + 1), "ry%d" % (t + 1))
+        tt(r("QY", 1, 129), r("YV"), r(X, 15, 2048, 16), O.subtract)
+        tt(r(XS, 0, 2048, 16), r("YV"), r("QY", 0, 128), O.subtract)
+        mm(r("S1", 0, 144), r("ONF", 0, 128, 1, 8), r("K2R", 0, 144, 1, 8), True, False)
+        for c in range(CH):
+            scan(ck("ED", c), ck(XS, c), ck(X, c), 0.0 if c == 0 else r("ED", 512 * c - 1, 512 * c), O.add, O.subtract)
+            act(ck("EA", c), ck("ED", c), F.Abs)
+        for k in range(16):
+            mm(r("S1", 1 + k, 136, 17), r("EA", k, 2048, 16), r("SR"), False, k == 15)
+
+    def count():
+        cn, dm = r("CN"), r("DM")
+        op("v", lambda e: e.tensor_reduce(out=cn[0], in_=dm[0], axis=AxisListType.X, op=O.add), [cn], [dm])
+        mm(r("D0", 0, 1), r("ONF", 0, 128), r("CN"), True, True)
+        cp(r("CI"), r("D0", 0, 1))
+        ts(r("CJ"), r("CI"), 31, O.bitwise_and)
+        tt(r("THC"), r("CJ"), r("TH"), O.add)
+        ts(r("SBI"), r("THC"), -1.0, O.mult, 0.5, O.add)
+
+    def ask1(t):
+        cp(r("K2S"), r("S1", 0, 144), "s")
+        scan(r("M1"), r("KMX"), r("K2S"), 0.0, O.min, O.max)
+        tt(r("DD", 1, 144), r("K2S", 1, 144), r("M1", 0, 143), O.min)
+        gather("v", r("OA"), r("M1"), r("L17"), r("K2S"), O.is_equal)
+        scan(r("M2"), r("KMX"), r("DD"), 0.0, O.min, O.max)
+        tt(r("OAV"), r("OA"), r("VT"), O.mult)
+        gather("v", r("OB"), r("M2"), r("L17"), r("K2S"), O.is_equal)
+        ts(r("ND"), r("M2"), 1.0, O.is_lt, r("DCOL"), O.mult)
+        tt(r("OBV"), r("OB"), r("VT"), O.mult)
+        scan(r("VA"), r("KMX"), r("OAV"), 0.0, O.min, O.max)
+        scan(r("VB"), r("KMX"), r("OBV"), 0.0, O.min, O.max)
+        gather("s", r("VAF"), r("VA"), r("LC"))
+        tt(r("OFS"), r("ND"), r("VB"), O.max)
+        gather("v", r("OFF"), r("OFS"), r("LC"))
+        gather("v", r("OFM"), r("OFS"), r("LC"), r("MASKJ"), O.mult)
+        mm(r("D0", 0, 128), r("OFF"), r("IDF"), True, True)
+        mm(r("D0", 128, 136), r("OFM"), r("RSEL"), True, True)
+        mm(r("D1", 0, 128), r("VAF"), r("IDF"), True, True)
+        if t < 3:
+            act(r("DW"), r("D1", 0, 128), F.Identity, 0.0, r("C1"))
+        cp(r("D32"), r("D1", 0, 128), "s")
+
+    def ask2(t):
+        for c in range(8):
+            ts(r("EQ", 128 * c + 112 - 16 * c, 128 * c + 128), r("D0", 0, 16 * c + 16), r("D0", 128 + c, 129 + c), O.is_equal)
+        if t < 3:
+            ts(r("DR"), r("D1", 0, 128), MAG64, O.add, MAG64, O.subtract)
+        scan(r("ST"), r("GRO"), r("EQ"), 0.0, O.mult, O.max)
+        if t < 3:
+            tt(r("DB"), r("DW"), r("DR"), O.subtract)
+        ts(r("LO"), r("ST", 127, 1024, 128), r("THR"), O.is_ge)
+        tt(r("LO2"), r("LO"), r("DUM"), O.mult)
+        tt(r("OFL"), r("LO2"), r("D0", 128, 136), O.max)
+        cp(r("OFU"), r("OFL"))
+        if t < 3:
+            scatter(r("TB"), r("OFU"), r("DB"))
+
+    start()
+    names(0)
+    hashes(0)
+    claims(0)
+    constants()
+    for t in range(4):
+        main(t)
+        landed("VU%d" % (t + 1), "rv%d" % (t + 1))
+        landed("YH%d" % (t + 1), "ry%d" % (t + 1))
+        if t < 3:
+            names(t + 1)
+            hashes(t + 1)
+            ask1(t)
+            claims(t + 1)
+            ask2(t)
+            scatter(r("T32"), r("OFU"), r("D32"))
+        else:
+            cp(r("YVF"), r("VU4"))
+            dma("y", inp(T.yv[:], "yv"), r("YVF"))
+            ask1(t)
+            ask2(t)
+            scatter(r("T32"), r("OFU"), r("D32"))
+            dma("y", inp(T.yp[:], "yp"), (T.T32[0:128:16, 0:8192], "T32", 0, 8192))
+            ts(r("YEB"), r("YH4"), -1024.0, O.add)
+            dma("s", inp(T.ye[:], "ye"), r("YEB"))
+    for s in sorted(tot):
+        g.wait_ge(T.sem[s], tot[s])

@@ -22,7 +22,7 @@ for _n, _c, _d in [
         ("OB", 144, F4), ("OA", 144, F4), ("OBV", 144, F4), ("OAV", 144, F4), ("VB", 144, F4), ("VA", 144, F4),
         ("ND", 144, F4), ("OFS", 144, F4), ("OFF", 128, F4), ("OFM", 128, F4), ("VAF", 128, F4), ("D32", 128, F4), ("DR", 128, F4), ("DW", 128, F4), ("DB", 128, BF),
         ("L16", 8, U2), ("LC", 8, U2), ("L17", 9, U2), ("LI16", 8, F4), ("LIC", 9, F4), ("CI9", 9, F4), ("CG9", 9, F4), ("LS9", 9, F4), ("IDW", 144, F4),
-        ("EQ", 1024, BF), ("ST", 1024, BF), ("LO", 8, F4), ("LO2", 8, F4), ("OFL", 8, F4), ("OFU", 8, U2),
+        ("SR2", 8, BF), ("NY", 144, BF), ("NY1", 136, BF), ("EQ", 1024, BF), ("ST", 1024, BF), ("LO", 8, F4), ("LO2", 8, F4), ("OFL", 8, F4), ("OFU", 8, U2),
         ("CN", 1, F4), ("CI", 1, I4), ("CJ", 1, I4), ("THC", 1, F4), ("SBI", 1, F4), ("TH", 1, F4),
         ("ONB", 512, BF), ("ONF", 256, F4), ("IDB", 128, BF), ("IDP", 128, BF), ("IDN", 128, BF), ("IDF", 128, F4),
         ("BK0", 128, BF), ("BLK", 128, BF), ("BL8", 8, BF), ("SR", 8, BF), ("DK", 2048, BF), ("EK", 2048, BF), ("WB", 128, H2), ("WC1", 1, F4), ("WC2", 1, F4), ("WCE", 1, F4), ("C1", 1, F4),
@@ -58,6 +58,7 @@ NS = 8
 CH = 4
 QX = "ssss"
 QP = "svsv"
+QF = "ssvv"
 CUT = 2
 MAG16, MAG64 = 1.5 * 2.0 ** 27, 1.5 * 2.0 ** 29
 
@@ -231,10 +232,13 @@ def rank_program(g, core, T, topo):
         aff(r("IDB"), r("ONB", 0, 128), [[-1, 128]], O.is_equal, 0.0, 0, 1)
         ms(r("NK"), -1024.0)
         ms(r("DK"), 0.0)
+        cp(r("BL8"), r("BLK", 0, 128, 16))
+        for k in range(16):
+            cp(r("DK", 128 * k + k, 128 * k + 128, 16), r("BL8"), "s")
         ms(r("TB"), 0.0)
         cp(r("PF"), r("PAR"))
         ts(r("P64"), r("PF"), MAG64, O.add, MAG64, O.subtract)
-        ts(r("PH"), r("P64"), -1.0, O.mult)
+        act(r("PH"), r("P64"), F.Copy, 0.0, -1.0)
         tt(r("PL"), r("PF"), r("P64"), O.subtract)
         dma("y", (T.TB[1:128:16, 0:8192], "TB", 0, 8192), r("PH"))
         dma("s", (T.TB[2:128:16, 0:8192], "TB", 0, 8192), r("PL"))
@@ -246,18 +250,14 @@ def rank_program(g, core, T, topo):
         cp(r("NKH"), r("NK"))
         mm(r("S0", 496, 497), r("WB"), r("NKH"), True, True)
         cp(r("CW"), r("S0", 496, 497))
-        cp(r("BL8"), r("BLK", 0, 128, 16))
         ts(r("PI5"), r("PI4"), 15, O.bitwise_and)
         cp(r("PM"), r("PI5"))
 
     def constants():
-        for k in range(16):
-            cp(r("DK", 128 * k + k, 128 * k + 128, 16), r("BL8"), "s")
         ts(r("WC1"), r("PM"), 1.0, O.is_equal)
         ts(r("WC2"), r("PM"), 2.0, O.is_equal)
         tt(r("WCE"), r("WC2"), r("WC1"), O.subtract)
         ts(r("EK"), r("DK"), r("WCE"), O.mult)
-        ts(r("C1"), r("PM"), 1.0, O.not_equal)
         cp(r("LF", 0, 2, 1, 8), r("LI", 0, 2, 1, 8))
         ts(r("N16", 0, 1, 1, 8), r("LF", 1, 2, 1, 8), -16.0, O.mult)
         mm(r("S0", 498, 499), r("SEL8", 0, 128, 1, 8), r("LF", 0, 1, 1, 8), True, True)
@@ -266,14 +266,11 @@ def rank_program(g, core, T, topo):
         ts(r("SBI"), r("TH"), -1.0, O.mult, 0.5, O.add)
         ts(r("IDP"), r("IDB"), 128.0, O.mult)
         ts(r("IDN"), r("IDB"), -128.0, O.mult)
-        cp(r("IDF"), r("IDB"))
-        ts(r("SR"), r("BL8"), 16.0, O.mult)
-        cp(r("RSEL"), r("BL8"))
-        ts(r("NRS"), r("RSEL"), -1.0, O.mult)
-        ts(r("PM16"), r("PM"), 16.0, O.mult)
         ms(r("IDW"), 0.0)
         aff(r("IW"), r("ONF", 0, 136), [[-16, 8], [-1, 17]], O.is_equal, 0.0, 1, 1)
         aff(r("IDW", 0, 136), r("IW"), [[0, 8], [1, 17]], O.is_gt, 0.0, 0, 0)
+
+    def constants_b():
         ms(r("RMX"), 1024.0)
         ms(r("RMX", 0, 512, 16), -1024.0)
         ms(r("RMN"), -1024.0)
@@ -282,26 +279,40 @@ def rank_program(g, core, T, topo):
         ms(r("QY", 0, 1), 0.0)
         iota(r("JI"), [[0, 8], [1, 16]], 0, 0)
         ts(r("KC"), r("JI"), -7.5, O.add)
-        ts(r("MASKJ"), r("JI"), r("PM"), O.is_equal)
         ts(r("PEN"), r("IDB"), 65536.0, O.mult)
+        ts(r("SR"), r("BL8"), 16.0, O.mult)
+        ts(r("SR2"), r("BL8"), 32.0, O.mult)
+        ms(r("NY"), -16.0)
+        aff(r("NY1"), r("NY", 0, 136), [[-16, 8], [0, 17]], O.is_ge, 0.0, 0, 1)
+        aff(r("NY", 0, 136), r("NY1"), [[16, 8], [0, 17]], O.is_ge, 0.0, 15, -1)
+        iota(r("KI"), [[0, 8], [1, 17]], 0, 0)
+
+    def constants_c():
+        ts(r("MASKJ"), r("JI"), r("PM"), O.is_equal)
+        cp(r("IDF"), r("IDB"))
+        cp(r("RSEL"), r("BL8"))
+        ts(r("NRS"), r("RSEL"), -1.0, O.mult)
+        ts(r("PM16"), r("PM"), 16.0, O.mult)
         iota(r("LI16"), [[16, 8]], 15, 0)
         cp(r("L16"), r("LI16"))
-        iota(r("LIC"), [[17, 9]], 16, 0)
-        cp(r("LC"), r("LIC", 0, 8))
-        iota(r("CI9"), [[1, 9]], 0, 0)
-        ts(r("CG9"), r("CI9"), r("PM"), O.is_gt, -17.0, O.mult)
-        tt(r("LS9"), r("LIC"), r("CG9"), O.add)
-        ts(r("L17"), r("LS9"), 143.0, O.min)
         iota(r("L0"), [[256, 8]], 0, 0)
         ts(r("LBASE"), r("L0"), r("PM16"), O.add, 7.5, O.add)
         ms(r("KMN"), -8388608.0)
         ms(r("KMN", 0, 128, 16), 8388608.0)
-        iota(r("KI"), [[0, 8], [1, 17]], 0, 0)
         ts(r("KN"), r("KI"), -1.0, O.mult, 17.0, O.add)
         aff(r("KN2"), r("KN"), [[0, 8], [1, 17]], O.is_gt, -4194304.0, 0, 0)
         ts(r("K2T", 0, 136, 1, 8), r("KN2", 0, 136, 1, 8), r("N16", 0, 1, 1, 8), O.add)
         ms(r("K2R"), 0.0)
         aff(r("K2R", 0, 136, 1, 8), r("K2T", 0, 136, 1, 8), [[-1, 8], [0, 17]], O.is_equal, 0.0, 0, 1)
+
+    def constants_d():
+        ts(r("C1"), r("PM"), 1.0, O.not_equal)
+        iota(r("LIC"), [[17, 9]], 16, 0)
+        iota(r("CI9"), [[1, 9]], 0, 0)
+        cp(r("LC"), r("LIC", 0, 8))
+        ts(r("CG9"), r("CI9"), r("PM"), O.is_gt, -17.0, O.mult)
+        tt(r("LS9"), r("LIC"), r("CG9"), O.add)
+        ts(r("L17"), r("LS9"), 143.0, O.min)
         ms(r("KMX"), 8388608.0)
         ms(r("KMX", 0, 144, 17), -8388608.0)
         ms(r("DD"), -8388608.0)
@@ -341,6 +352,8 @@ def rank_program(g, core, T, topo):
         X, XS, VF, UQ = "X%d" % p, "XS%d" % p, "VF%d" % p, "UQ%d" % p
         R, R2 = ["R0", "R1", "R2", "R3"], ["D0", "D1", "R0", "R1"]
         to = rank + (3 if t < 3 else -9)
+        mm(r("S1", 128, 272), r(VF), r("IDW"), True, True)
+        cp(r("VT"), r("S1", 128, 272), "s")
         for c in range(CH):
             gather(QP[c], ck("PG", c), r("TB", 0, 8192), lk("VU%d" % t, c))
 
@@ -348,40 +361,75 @@ def rank_program(g, core, T, topo):
             mm(r(R[c]), r("IDP"), ck("SG", c), False, True)
 
         def turned(c):
-            mm(r(R2[c]), r("IDB"), ck(X, c), True, False)
             mm(r(R2[c]), r("IDN"), ck("SG", c), False, True)
+
+        def plain(c):
+            mm(r(R2[c]), r("IDB"), ck(X, c), True, False)
 
         for c in range(CH):
             mm(r(R[c]), r("IDB"), ck(X, c), True, False)
-        for h in range(CUT):
-            w = 128 // CUT
-            a, b = w * h, w * h + w
+        if t:
+            count2()
+        PP = [r("S0", 128, 192), r("S1", 288, 352)]
+        for h in range(2):
             for k in range(16):
-                mm(r("S0", 128 + a, 128 + b), r("EK", 128 * k, 128 * k + 128), r("PG", 16 * a + k, 16 * b, 16), k == 0, k == 15)
-            tt(r("PA", a, b), r("S0", 128 + a, 128 + b), r(UQ, a, b), O.mult)
-            act(r("S3P", a, b), r("S0", 128 + a, 128 + b), F.Copy, 32.0 * 77 * t - 262144.0, 32.0)
+                mm(PP[h], r("EK", 128 * k, 128 * k + 128), r("PG", 1024 * h + k, 1024 * h + 1024, 16), k == 0, k == 15)
+
+        def hashp(h):
+            a, b = 64 * h, 64 * h + 64
+            tt(r("PA", a, b), PP[h], r(UQ, a, b), O.mult)
             tt(r("PB", a, b), r("PA", a, b), r("S3P", a, b), O.add)
             ts(r("PC", a, b), r("PB", a, b), 5, O.arith_shift_right, 8191, O.bitwise_and)
             cp(r("HZ", a, b), r("PC", a, b))
-            for c in range(CH * h // CUT, CH * (h + 1) // CUT):
-                gather("v", ck("DZ", c), r("CL"), lk("HZ", c), ck(X, c), O.subtract)
-                act(ck("AD", c), ck("DZ", c), F.Abs)
-                mm(r("D%d" % (c & 1)), r("BLK"), ck("AD", c), True, True)
-                act(ck("SG", c), r("D%d" % (c & 1)), F.Sign, r("SBI"))
-                if c:
-                    masked(c - 1)
-        masked(CH - 1)
+
+        def dist(c):
+            gather("v", ck("DZ", c), r("CL"), lk("HZ", c), ck(X, c), O.subtract)
+            act(ck("AD", c), ck("DZ", c), F.Abs)
+
+        def total(c):
+            mm(r("D%d" % (c & 1)), r("BLK"), ck("AD", c), True, True)
+
+        def sign(c):
+            act(ck("SG", c), r("D%d" % (c & 1)), F.Sign, r("SBI"))
+
+        for h in range(2):
+            act(r("S3P", 64 * h, 64 * h + 64), PP[h], F.Copy, 32.0 * 77 * t - 262144.0, 32.0)
+        hashp(0)
+        dist(0)
+        total(0)
+        dist(1)
+        total(1)
+        hashp(1)
+        sign(0)
+        dist(2)
+        masked(0)
+        total(2)
+        sign(1)
+        dist(3)
+        masked(1)
+        total(3)
+        sign(2)
+        plain(0)
+        masked(2)
+        sign(3)
+        masked(3)
         turned(0)
+        plain(1)
         turned(1)
-        tt(r("PV"), r("S0", 128, 256), r(VF), O.subtract)
+        if t == 0:
+            constants_b()
+        else:
+            scatter(r("T32"), r("OFU"), r("D32"))
+        for h in range(2):
+            tt(r("PV", 64 * h, 64 * h + 64), PP[h], r(VF, 64 * h, 64 * h + 64), O.subtract)
         shifted(t)
         for c in range(CH):
             scan(ck("SA", c), r("RMX"), r(R[c]), 0.0, O.min, O.max)
             if c < 2:
+                plain(c + 2)
                 turned(c + 2)
         for k in range(16):
-            mm(r("S1", 0, 128), r("DK", 128 * k, 128 * k + 128), r("AD", k, 2048, 16), k == 0, k == 15)
-        mm(r("S1", 128, 272), r(VF), r("IDW"), True, True)
+            mm(r("R3", 0, 128), r("DK", 128 * k, 128 * k + 128), r("AD", k, 2048, 16), k == 0, k == 15)
         for c in range(CH):
             scan(ck("SB", c), r("RMN"), r(R2[c]), 0.0, O.max, O.min)
         tt(r("SS"), r("SA", 15, 2048, 16), r("SB", 15, 2048, 16), O.add)
@@ -390,26 +438,35 @@ def rank_program(g, core, T, topo):
         tt(r(XS, 0, 2048, 16), r("MH"), r("QP", 0, 128), O.subtract)
         for c in range(CH):
             scan(ck("FD", c), ck(XS, c), ck(X, c), -1024.0 if c == 0 else r("FD", 512 * c - 1, 512 * c), O.add, O.subtract)
-            act(ck("FA", c), ck("FD", c), F.Abs)
-        ts(r("DM"), r("S1", 0, 128), r("THC"), O.is_lt)
-        cp(r("VT"), r("S1", 128, 272), "s")
+            if QF[c] == "s":
+                act(ck("FA", c), ck("FD", c), F.Relu)
+        for c in range(CH):
+            if QF[c] == "v":
+                ts(ck("FA", c), ck("FD", c), 0.0, O.max)
+        ts(r("DM"), r("R3", 0, 128), r("THC"), O.is_lt)
+        if t < 3:
+            count1()
+        if t == 0:
+            constants_c()
         mm(r("S1", 0, 128), r("ONB", 0, 128, 1, 1), r("KC", 0, 128, 1, 1), True, False)
+        for k in range(16):
+            mm(r("S1", k, 128, 16), r(X, k, 2048, 16), r("SR"), False, False)
+        mm(r("S0", 256, 264), r("IDF"), r("LBASE"), True, False)
         mm(r("S1", 0, 128), r("DM"), r("PEN"), False, False)
         for k in range(16):
-            mm(r("S1", k, 128, 16), r("FA", k, 2048, 16), r("SR"), False, k == 15)
-        mm(r("S0", 256, 264), r("IDF"), r("LBASE"), True, False)
+            mm(r("S1", k, 128, 16), r("FA", k, 2048, 16), r("SR2"), False, k == 15)
         tt(r("DP"), r("PV"), r("DM"), O.mult)
         tt(r("VN"), r("DP"), r(VF), O.add)
         cp(r("VO%d" % t), r("VN"))
         send(to, r("VO%d" % t), "VU%d" % (t + 1), "rv%d" % (t + 1))
-        if t < 3:
-            count()
         scan(r("MN"), r("KMN"), r("S1", 0, 128), 0.0, O.max, O.min)
         gather("v", r("MM"), r("MN"), r("L16"), r("MASKJ"), O.mult)
         mm(r("S0", 256, 264), r("MM"), r("RSEL"), False, False)
         ts(r("MR"), r("MM"), MAG16, O.add, MAG16, O.subtract)
         mm(r("S0", 256, 264), r("MR"), r("NRS"), False, True)
         cp(r("YL"), r("S0", 256, 264))
+        if t < 3:
+            mm(r("S0", 400, 401), r("ONF", 0, 128), r("CN"), True, True)
         gather("s", r("YV"), r(X), r("YL"))
         gather("v", r("YS"), r(X), r("YL"), r("YH%d" % t), O.add)
         ts(r("YO%d" % t), r("YS"), 0.5, O.mult, 511.8, O.add)
@@ -417,39 +474,53 @@ def rank_program(g, core, T, topo):
         tt(r("QY", 1, 129), r("YV"), r(X, 15, 2048, 16), O.subtract)
         tt(r(XS, 0, 2048, 16), r("YV"), r("QY", 0, 128), O.subtract)
         mm(r("S1", 0, 144), r("ONF", 0, 128, 1, 8), r("K2R", 0, 144, 1, 8), True, False)
+        for k in range(16):
+            mm(r("S1", 1 + k, 136, 17), r(X, k, 2048, 16), r("SR"), False, False)
+        mm(r("S1", 0, 144), r("YV"), r("NY"), False, False)
         for c in range(CH):
             scan(ck("ED", c), ck(XS, c), ck(X, c), 0.0 if c == 0 else r("ED", 512 * c - 1, 512 * c), O.add, O.subtract)
-            act(ck("EA", c), ck("ED", c), F.Abs)
-        for k in range(16):
-            mm(r("S1", 1 + k, 136, 17), r("EA", k, 2048, 16), r("SR"), False, k == 15)
+            if QF[c] == "s":
+                act(ck("EA", c), ck("ED", c), F.Relu)
+        for c in range(CH):
+            if QF[c] == "v":
+                ts(ck("EA", c), ck("ED", c), 0.0, O.max)
+        if t == 0:
+            constants_d()
 
-    def count():
+    def errors(t):
+        for k in range(16):
+            mm(r("S1", 1 + k, 136, 17), r("EA", k, 2048, 16), r("SR2"), False, k == 15)
+
+    def count1():
         cn, dm = r("CN"), r("DM")
         op("v", lambda e: e.tensor_reduce(out=cn[0], in_=dm[0], axis=AxisListType.X, op=O.add), [cn], [dm])
-        mm(r("D0", 0, 1), r("ONF", 0, 128), r("CN"), True, True)
-        cp(r("CI"), r("D0", 0, 1))
+
+    def count2():
+        cp(r("CI"), r("S0", 400, 401))
         ts(r("CJ"), r("CI"), 31, O.bitwise_and)
         tt(r("THC"), r("CJ"), r("TH"), O.add)
         ts(r("SBI"), r("THC"), -1.0, O.mult, 0.5, O.add)
 
     def ask1(t):
+        scan(r("M1"), r("KMX"), r("S1", 0, 144), 0.0, O.min, O.max)
+        tt(r("DD", 1, 144), r("S1", 1, 144), r("M1", 0, 143), O.min)
         cp(r("K2S"), r("S1", 0, 144), "s")
-        scan(r("M1"), r("KMX"), r("K2S"), 0.0, O.min, O.max)
-        tt(r("DD", 1, 144), r("K2S", 1, 144), r("M1", 0, 143), O.min)
-        gather("v", r("OA"), r("M1"), r("L17"), r("K2S"), O.is_equal)
+        if t < 3:
+            claims(t + 1)
         scan(r("M2"), r("KMX"), r("DD"), 0.0, O.min, O.max)
-        tt(r("OAV"), r("OA"), r("VT"), O.mult)
         gather("v", r("OB"), r("M2"), r("L17"), r("K2S"), O.is_equal)
         ts(r("ND"), r("M2"), 1.0, O.is_lt, r("DCOL"), O.mult)
         tt(r("OBV"), r("OB"), r("VT"), O.mult)
-        scan(r("VA"), r("KMX"), r("OAV"), 0.0, O.min, O.max)
         scan(r("VB"), r("KMX"), r("OBV"), 0.0, O.min, O.max)
-        gather("s", r("VAF"), r("VA"), r("LC"))
         tt(r("OFS"), r("ND"), r("VB"), O.max)
         gather("v", r("OFF"), r("OFS"), r("LC"))
         gather("v", r("OFM"), r("OFS"), r("LC"), r("MASKJ"), O.mult)
         mm(r("D0", 0, 128), r("OFF"), r("IDF"), True, True)
         mm(r("D0", 128, 136), r("OFM"), r("RSEL"), True, True)
+        gather("v", r("OA"), r("M1"), r("L17"), r("K2S"), O.is_equal)
+        tt(r("OAV"), r("OA"), r("VT"), O.mult)
+        scan(r("VA"), r("KMX"), r("OAV"), 0.0, O.min, O.max)
+        gather("v", r("VAF"), r("VA"), r("LC"))
         mm(r("D1", 0, 128), r("VAF"), r("IDF"), True, True)
         if t < 3:
             act(r("DW"), r("D1", 0, 128), F.Identity, 0.0, r("C1"))
@@ -482,13 +553,13 @@ def rank_program(g, core, T, topo):
         if t < 3:
             names(t + 1)
             hashes(t + 1)
+            errors(t)
             ask1(t)
-            claims(t + 1)
             ask2(t)
-            scatter(r("T32"), r("OFU"), r("D32"))
         else:
             cp(r("YVF"), r("VU4"))
             dma("y", inp(T.yv[:], "yv"), r("YVF"))
+            errors(t)
             ask1(t)
             ask2(t)
             scatter(r("T32"), r("OFU"), r("D32"))

@@ -11,20 +11,20 @@ def _b(name, cols, dtype="float32", where="sbuf"):
 
 for _n, _c, _d in [
         ("CL", 8192, BF), ("TB", 8320, BF), ("T32", 8320, F4),
-        ("X0", 2048, BF), ("X1", 2048, BF), ("XS0", 2064, H2), ("XS1", 2064, H2),
+        ("X0", 2048, BF), ("X1", 2048, BF), ("XS0", 2064, BF), ("XS1", 2064, BF), ("XM0", 2048, BF), ("XM1", 2048, BF),
         ("PG", 2048, BF), ("DZ", 2048, BF), ("AD", 2048, BF), ("SG", 2048, BF),
         ("SA", 2048, F4), ("SB", 2048, F4), ("FD", 2048, BF), ("FA", 2048, BF), ("ED", 2048, BF), ("EA", 2048, BF),
         ("VF0", 128, F4), ("VF1", 128, F4), ("S32", 128, F4), ("UI", 128, I4), ("UQ0", 128, I4), ("UQ1", 128, I4), ("HA", 128, F4), ("HB", 128, I4), ("HC", 128, I4), ("HX", 128, U2),
         ("S3P", 128, F4), ("PA", 128, F4), ("PB", 128, I4), ("PC", 128, I4), ("HZ", 128, U2),
         ("PV", 128, F4), ("DP", 128, F4), ("VN", 128, F4), ("DM", 128, BF), ("VT", 144, F4),
-        ("SS", 128, F4), ("MH", 128, H2), ("QP", 136, F4), ("QY", 136, F4), ("YV", 128, BF), ("YS", 128, F4), ("YL", 8, U2),
+        ("SS", 128, F4), ("MH", 136, H2), ("YV", 136, BF), ("YS", 128, F4), ("YL", 8, U2),
         ("MN", 128, F4), ("MM", 128, F4), ("MR", 128, F4), ("K2S", 144, F4), ("M1", 144, F4), ("M2", 144, F4), ("DD", 144, F4),
         ("OB", 144, F4), ("OA", 144, F4), ("OBV", 144, F4), ("OAV", 144, F4), ("VB", 144, F4), ("VA", 144, F4),
         ("ND", 144, F4), ("OFS", 144, F4), ("OFF", 128, F4), ("OFM", 128, F4), ("VAF", 128, F4), ("D32", 128, F4), ("DR", 128, F4), ("DW", 128, F4), ("DB", 128, BF),
         ("L16", 8, U2), ("LC", 8, U2), ("L17", 9, U2), ("LI16", 8, F4), ("LIC", 9, F4), ("CI9", 9, F4), ("CG9", 9, F4), ("LS9", 9, F4), ("IDW", 144, F4),
         ("SR2", 8, BF), ("NY", 144, BF), ("NY1", 136, BF), ("EQ", 1024, BF), ("ST", 1024, BF), ("LO", 8, F4), ("LO2", 8, F4), ("OFL", 8, F4), ("OFU", 8, U2),
         ("CN", 1, F4), ("CI", 1, I4), ("CJ", 1, I4), ("THC", 1, F4), ("SBI", 1, F4), ("TH", 1, F4),
-        ("ONB", 512, BF), ("ONF", 256, F4), ("IDB", 128, BF), ("IDP", 128, BF), ("IDN", 128, BF), ("IDF", 128, F4),
+        ("ONB", 512, BF), ("ONF", 256, F4), ("IDB", 128, BF), ("IDP", 128, BF), ("IDN", 128, BF), ("IDP2", 128, BF), ("IDN2", 128, BF), ("X15", 128, F4), ("INI", 3, F4), ("INY", 3, F4), ("IDF", 128, F4),
         ("BK0", 128, BF), ("BLK", 128, BF), ("BL8", 8, BF), ("SR", 8, BF), ("DK", 2048, BF), ("EK", 2048, BF), ("WB", 128, H2), ("WC1", 1, F4), ("WC2", 1, F4), ("WCE", 1, F4), ("C1", 1, F4),
         ("PI4", 1, I4), ("PI5", 1, I4), ("PM", 1, F4), ("PM16", 1, F4), ("DCOL", 1, F4), ("THR", 1, F4), ("THB", 1, F4),
         ("PEN", 128, BF), ("KI", 136, F4), ("KC", 128, BF), ("KN", 136, F4), ("KN2", 136, F4), ("K2T", 136, F4), ("K2R", 144, F4), ("IW", 136, F4),
@@ -59,7 +59,7 @@ CH = 4
 QX = "ssss"
 QP = "svsv"
 QF = "ssvv"
-CUT = 2
+HS = 1
 MAG16, MAG64 = 1.5 * 2.0 ** 27, 1.5 * 2.0 ** 29
 
 
@@ -235,7 +235,9 @@ def rank_program(g, core, T, topo):
         cp(r("BL8"), r("BLK", 0, 128, 16))
         for k in range(16):
             cp(r("DK", 128 * k + k, 128 * k + 128, 16), r("BL8"), "s")
-        ms(r("TB"), 0.0)
+        ms(r("TB", 0, 5760), 0.0)
+        for c in range(5):
+            cp(r("TB", 5760 + 512 * c, 6272 + 512 * c), r("ONB"), "s")
         cp(r("PF"), r("PAR"))
         ts(r("P64"), r("PF"), MAG64, O.add, MAG64, O.subtract)
         act(r("PH"), r("P64"), F.Copy, 0.0, -1.0)
@@ -266,6 +268,8 @@ def rank_program(g, core, T, topo):
         ts(r("SBI"), r("TH"), -1.0, O.mult, 0.5, O.add)
         ts(r("IDP"), r("IDB"), 128.0, O.mult)
         ts(r("IDN"), r("IDB"), -128.0, O.mult)
+        ts(r("IDP2"), r("IDB"), 256.0, O.mult)
+        ts(r("IDN2"), r("IDB"), -256.0, O.mult)
         ms(r("IDW"), 0.0)
         aff(r("IW"), r("ONF", 0, 136), [[-16, 8], [-1, 17]], O.is_equal, 0.0, 1, 1)
         aff(r("IDW", 0, 136), r("IW"), [[0, 8], [1, 17]], O.is_gt, 0.0, 0, 0)
@@ -275,8 +279,8 @@ def rank_program(g, core, T, topo):
         ms(r("RMX", 0, 512, 16), -1024.0)
         ms(r("RMN"), -1024.0)
         ms(r("RMN", 0, 512, 16), 1024.0)
-        ms(r("QP", 0, 1), 0.0)
-        ms(r("QY", 0, 1), 0.0)
+        ts(r("MH", 0, 1), r("NK"), -1.0, O.mult)
+        ms(r("YV", 0, 1), 0.0)
         iota(r("JI"), [[0, 8], [1, 16]], 0, 0)
         ts(r("KC"), r("JI"), -7.5, O.add)
         ts(r("PEN"), r("IDB"), 65536.0, O.mult)
@@ -286,6 +290,20 @@ def rank_program(g, core, T, topo):
         aff(r("NY1"), r("NY", 0, 136), [[-16, 8], [0, 17]], O.is_ge, 0.0, 0, 1)
         aff(r("NY", 0, 136), r("NY1"), [[16, 8], [0, 17]], O.is_ge, 0.0, 15, -1)
         iota(r("KI"), [[0, 8], [1, 17]], 0, 0)
+        iota(r("LI16"), [[16, 8]], 15, 0)
+        iota(r("L0"), [[256, 8]], 0, 0)
+        iota(r("LIC"), [[17, 9]], 16, 0)
+        iota(r("CI9"), [[1, 9]], 0, 0)
+        iota(r("DCOL"), [[0, 1]], 8192, 1)
+        iota(r("DU0"), [[16, 8]], 8192, 0)
+        ms(r("KMX"), 8388608.0)
+        ms(r("DD"), -8388608.0)
+        ms(r("KMX", 0, 144, 17), -8388608.0)
+        ms(r("GRO"), 1.5)
+        ms(r("EQ"), 0.0)
+        ms(r("GRO", 0, 1024, 128), 0.0)
+        ts(r("KN"), r("KI"), -1.0, O.mult, 17.0, O.add)
+        aff(r("KN2"), r("KN"), [[0, 8], [1, 17]], O.is_gt, -4194304.0, 0, 0)
 
     def constants_c():
         ts(r("MASKJ"), r("JI"), r("PM"), O.is_equal)
@@ -293,37 +311,34 @@ def rank_program(g, core, T, topo):
         cp(r("RSEL"), r("BL8"))
         ts(r("NRS"), r("RSEL"), -1.0, O.mult)
         ts(r("PM16"), r("PM"), 16.0, O.mult)
-        iota(r("LI16"), [[16, 8]], 15, 0)
         cp(r("L16"), r("LI16"))
-        iota(r("L0"), [[256, 8]], 0, 0)
         ts(r("LBASE"), r("L0"), r("PM16"), O.add, 7.5, O.add)
         ms(r("KMN"), -8388608.0)
         ms(r("KMN", 0, 128, 16), 8388608.0)
-        ts(r("KN"), r("KI"), -1.0, O.mult, 17.0, O.add)
-        aff(r("KN2"), r("KN"), [[0, 8], [1, 17]], O.is_gt, -4194304.0, 0, 0)
         ts(r("K2T", 0, 136, 1, 8), r("KN2", 0, 136, 1, 8), r("N16", 0, 1, 1, 8), O.add)
         ms(r("K2R"), 0.0)
         aff(r("K2R", 0, 136, 1, 8), r("K2T", 0, 136, 1, 8), [[-1, 8], [0, 17]], O.is_equal, 0.0, 0, 1)
 
     def constants_d():
         ts(r("C1"), r("PM"), 1.0, O.not_equal)
-        iota(r("LIC"), [[17, 9]], 16, 0)
-        iota(r("CI9"), [[1, 9]], 0, 0)
         cp(r("LC"), r("LIC", 0, 8))
         ts(r("CG9"), r("CI9"), r("PM"), O.is_gt, -17.0, O.mult)
         tt(r("LS9"), r("LIC"), r("CG9"), O.add)
         ts(r("L17"), r("LS9"), 143.0, O.min)
-        ms(r("KMX"), 8388608.0)
-        ms(r("KMX", 0, 144, 17), -8388608.0)
-        ms(r("DD"), -8388608.0)
-        iota(r("DCOL"), [[0, 1]], 8192, 1)
-        iota(r("DU0"), [[16, 8]], 8192, 0)
         ts(r("DUM"), r("DU0"), r("PM"), O.add)
-        ms(r("GRO"), 1.5)
-        ms(r("GRO", 0, 1024, 128), 0.0)
-        ms(r("EQ"), 0.0)
         ms(r("THB"), 6.3051201)
         act(r("THR"), r("PM"), F.Exp, r("THB"), -0.4054651)
+
+    def run(steps, others):
+        others = [list(o) for o in others]
+        for f in steps:
+            f()
+            for o in others:
+                if o:
+                    o.pop(0)()
+        for o in others:
+            for f in o:
+                f()
 
     def names(t):
         cp(r("VF%d" % (t & 1)), r("VU%d" % t))
@@ -332,44 +347,43 @@ def rank_program(g, core, T, topo):
     def hashes(t):
         UQ = "UQ%d" % (t & 1)
         mm(r("S0", 0, 128), r("WB"), r("YH%d" % t), True, True)
-        ts(r("UI"), r("S0", 0, 128), r("CW"), O.add)
-        ts(r(UQ), r("UI"), 2047, O.bitwise_and)
-        tt(r("HA"), r("VF%d" % (t & 1)), r(UQ), O.mult)
-        tt(r("HB"), r("HA"), r("S32"), O.add)
-        ts(r("HC"), r("HB"), 5, O.arith_shift_right, 8191, O.bitwise_and)
-        cp(r("HX"), r("HC"))
+        return [lambda: ts(r("UI"), r("S0", 0, 128), r("CW"), O.add),
+                lambda: ts(r(UQ), r("UI"), 2047, O.bitwise_and),
+                lambda: tt(r("HA"), r("VF%d" % (t & 1)), r(UQ), O.mult),
+                lambda: tt(r("HB"), r("HA"), r("S32"), O.add),
+                lambda: ts(r("HC"), r("HB"), 5, O.arith_shift_right, 8191, O.bitwise_and),
+                lambda: cp(r("HX"), r("HC"))]
 
-    def claims(t):
-        for c in range(CH):
+    def claims(t, a=0, b=CH):
+        for c in range(a, b):
             gather(QX[c], ck("X%d" % (t & 1), c), r("CL"), lk("HX", c))
 
     def shifted(t):
+        X, XS, XM = "X%d" % (t & 1), "XS%d" % (t & 1), "XM%d" % (t & 1)
         for c in range(CH):
-            cp(r("XS%d" % (t & 1), 512 * c + 1, 512 * c + 513), ck("X%d" % (t & 1), c))
+            aff(ck(XM, c), ck(X, c), [[0, 512]], O.is_gt, 0.0, 1, 0)
+        for c in range(CH):
+            aff(r(XS, 512 * c + 1, 512 * c + 513), ck(X, c), [[0, 512]], O.is_gt, 0.0, 1, 0)
 
     def main(t):
         p = t & 1
-        X, XS, VF, UQ = "X%d" % p, "XS%d" % p, "VF%d" % p, "UQ%d" % p
+        X, XS, XM, VF, UQ = "X%d" % p, "XS%d" % p, "XM%d" % p, "VF%d" % p, "UQ%d" % p
         R, R2 = ["R0", "R1", "R2", "R3"], ["D0", "D1", "R0", "R1"]
         to = rank + (3 if t < 3 else -9)
-        mm(r("S1", 128, 272), r(VF), r("IDW"), True, True)
-        cp(r("VT"), r("S1", 128, 272), "s")
         for c in range(CH):
-            gather(QP[c], ck("PG", c), r("TB", 0, 8192), lk("VU%d" % t, c))
+            gather(QP[c] if t else "s", ck("PG", c), r("TB", 0, 8192), lk("VU%d" % t, c))
 
         def masked(c):
-            mm(r(R[c]), r("IDP"), ck("SG", c), False, True)
+            mm(r(R[c]), r("IDP" if c < 3 else "IDP2"), ck("SG", c), False, True)
 
         def turned(c):
-            mm(r(R2[c]), r("IDN"), ck("SG", c), False, True)
+            mm(r(R2[c]), r("IDN" if c < 3 else "IDN2"), ck("SG", c), False, True)
 
         def plain(c):
             mm(r(R2[c]), r("IDB"), ck(X, c), True, False)
 
         for c in range(CH):
             mm(r(R[c]), r("IDB"), ck(X, c), True, False)
-        if t:
-            count2()
         PP = [r("S0", 128, 192), r("S1", 288, 352)]
         for h in range(2):
             for k in range(16):
@@ -377,10 +391,13 @@ def rank_program(g, core, T, topo):
 
         def hashp(h):
             a, b = 64 * h, 64 * h + 64
-            tt(r("PA", a, b), PP[h], r(UQ, a, b), O.mult)
-            tt(r("PB", a, b), r("PA", a, b), r("S3P", a, b), O.add)
-            ts(r("PC", a, b), r("PB", a, b), 5, O.arith_shift_right, 8191, O.bitwise_and)
-            cp(r("HZ", a, b), r("PC", a, b))
+            return [lambda: tt(r("PA", a, b), PP[h], r(UQ, a, b), O.mult),
+                    lambda: tt(r("PB", a, b), r("PA", a, b), r("S3P", a, b), O.add),
+                    lambda: ts(r("PC", a, b), r("PB", a, b), 5, O.arith_shift_right, 8191, O.bitwise_and),
+                    lambda: cp(r("HZ", a, b), r("PC", a, b))]
+
+        def change(h):
+            tt(r("PV", 64 * h, 64 * h + 64), PP[h], r(VF, 64 * h, 64 * h + 64), O.subtract)
 
         def dist(c):
             gather("v", ck("DZ", c), r("CL"), lk("HZ", c), ck(X, c), O.subtract)
@@ -394,12 +411,18 @@ def rank_program(g, core, T, topo):
 
         for h in range(2):
             act(r("S3P", 64 * h, 64 * h + 64), PP[h], F.Copy, 32.0 * 77 * t - 262144.0, 32.0)
-        hashp(0)
+        run(hashp(0), [])
+        first, second = hashp(1)[:2], hashp(1)[2:]
+        first[0]()
         dist(0)
         total(0)
+        first[1]()
         dist(1)
         total(1)
-        hashp(1)
+        second[0]()
+        change(0)
+        change(1)
+        second[1]()
         sign(0)
         dist(2)
         masked(0)
@@ -408,46 +431,48 @@ def rank_program(g, core, T, topo):
         dist(3)
         masked(1)
         total(3)
-        sign(2)
-        plain(0)
-        masked(2)
-        sign(3)
-        masked(3)
-        turned(0)
-        plain(1)
-        turned(1)
         if t == 0:
-            constants_b()
+            constants_c()
         else:
             scatter(r("T32"), r("OFU"), r("D32"))
-        for h in range(2):
-            tt(r("PV", 64 * h, 64 * h + 64), PP[h], r(VF, 64 * h, 64 * h + 64), O.subtract)
-        shifted(t)
+        sign(2)
+        masked(2)
+        plain(0)
+        turned(0)
+        ts(r("X15"), r(X, 15, 2048, 16), 1024.0, O.add)
+        tt(r(XM, 16, 2048, 16), r(X, 16, 2048, 16), r(X, 15, 2047, 16), O.subtract)
         for c in range(CH):
             scan(ck("SA", c), r("RMX"), r(R[c]), 0.0, O.min, O.max)
-            if c < 2:
-                plain(c + 2)
-                turned(c + 2)
+            if c == 1:
+                ts(ck("SG", 3), r("D1"), r("THC"), O.is_ge)
+                masked(3)
+                plain(2)
+                turned(2)
+                plain(1)
+                turned(1)
+                plain(3)
+                turned(3)
+        mm(r("R2", 0, 144), r(VF), r("IDW"), True, True)
         for k in range(16):
             mm(r("R3", 0, 128), r("DK", 128 * k, 128 * k + 128), r("AD", k, 2048, 16), k == 0, k == 15)
-        for c in range(CH):
+        for c in (0, 2, 1, 3):
             scan(ck("SB", c), r("RMN"), r(R2[c]), 0.0, O.max, O.min)
-        tt(r("SS"), r("SA", 15, 2048, 16), r("SB", 15, 2048, 16), O.add)
-        ts(r("MH"), r("SS"), 0.5, O.mult, 1023.8, O.add)
-        tt(r("QP", 1, 129), r("MH"), r(X, 15, 2048, 16), O.subtract)
-        tt(r(XS, 0, 2048, 16), r("MH"), r("QP", 0, 128), O.subtract)
+        run([lambda: tt(r("SS"), r("SA", 15, 2048, 16), r("SB", 15, 2048, 16), O.add),
+             lambda: ts(r("MH", 1, 129), r("SS"), 0.5, O.mult, 1023.8, O.add),
+             lambda: tt(r(XS, 0, 2048, 16), r("MH", 1, 129), r("MH", 0, 128), O.subtract)],
+            [[lambda: ts(r("DM"), r("R3", 0, 128), r("THC"), O.is_lt),
+              lambda: tt(r("DP"), r("PV"), r("DM"), O.mult),
+              lambda: tt(r("VN"), r("DP"), r(VF), O.add)]])
+        tt(r("INI"), r("MH", 32, 128, 32), r("X15", 31, 127, 32), O.subtract)
+        cp(r("VO%d" % t), r("VN"))
+        send(to, r("VO%d" % t), "VU%d" % (t + 1), "rv%d" % (t + 1))
         for c in range(CH):
-            scan(ck("FD", c), ck(XS, c), ck(X, c), -1024.0 if c == 0 else r("FD", 512 * c - 1, 512 * c), O.add, O.subtract)
+            scan(ck("FD", c), ck(XS, c), ck(XM, c), 0.0 if c == 0 else r("INI", c - 1, c), O.add, O.subtract)
             if QF[c] == "s":
                 act(ck("FA", c), ck("FD", c), F.Relu)
         for c in range(CH):
             if QF[c] == "v":
                 ts(ck("FA", c), ck("FD", c), 0.0, O.max)
-        ts(r("DM"), r("R3", 0, 128), r("THC"), O.is_lt)
-        if t < 3:
-            count1()
-        if t == 0:
-            constants_c()
         mm(r("S1", 0, 128), r("ONB", 0, 128, 1, 1), r("KC", 0, 128, 1, 1), True, False)
         for k in range(16):
             mm(r("S1", k, 128, 16), r(X, k, 2048, 16), r("SR"), False, False)
@@ -455,30 +480,28 @@ def rank_program(g, core, T, topo):
         mm(r("S1", 0, 128), r("DM"), r("PEN"), False, False)
         for k in range(16):
             mm(r("S1", k, 128, 16), r("FA", k, 2048, 16), r("SR2"), False, k == 15)
-        tt(r("DP"), r("PV"), r("DM"), O.mult)
-        tt(r("VN"), r("DP"), r(VF), O.add)
-        cp(r("VO%d" % t), r("VN"))
-        send(to, r("VO%d" % t), "VU%d" % (t + 1), "rv%d" % (t + 1))
         scan(r("MN"), r("KMN"), r("S1", 0, 128), 0.0, O.max, O.min)
         gather("v", r("MM"), r("MN"), r("L16"), r("MASKJ"), O.mult)
         mm(r("S0", 256, 264), r("MM"), r("RSEL"), False, False)
         ts(r("MR"), r("MM"), MAG16, O.add, MAG16, O.subtract)
         mm(r("S0", 256, 264), r("MR"), r("NRS"), False, True)
+        if t < 3:
+            count1()
         cp(r("YL"), r("S0", 256, 264))
         if t < 3:
             mm(r("S0", 400, 401), r("ONF", 0, 128), r("CN"), True, True)
-        gather("s", r("YV"), r(X), r("YL"))
         gather("v", r("YS"), r(X), r("YL"), r("YH%d" % t), O.add)
+        gather("v", r("YV", 1, 129), r(X), r("YL"))
         ts(r("YO%d" % t), r("YS"), 0.5, O.mult, 511.8, O.add)
         send(to, r("YO%d" % t), "YH%d" % (t + 1), "ry%d" % (t + 1))
-        tt(r("QY", 1, 129), r("YV"), r(X, 15, 2048, 16), O.subtract)
-        tt(r(XS, 0, 2048, 16), r("YV"), r("QY", 0, 128), O.subtract)
+        tt(r(XS, 0, 2048, 16), r("YV", 1, 129), r("YV", 0, 128), O.subtract)
+        tt(r("INY"), r("YV", 32, 128, 32), r(X, 511, 2047, 512), O.subtract)
         mm(r("S1", 0, 144), r("ONF", 0, 128, 1, 8), r("K2R", 0, 144, 1, 8), True, False)
         for k in range(16):
             mm(r("S1", 1 + k, 136, 17), r(X, k, 2048, 16), r("SR"), False, False)
-        mm(r("S1", 0, 144), r("YV"), r("NY"), False, False)
+        mm(r("S1", 0, 144), r("YV", 1, 129), r("NY"), False, False)
         for c in range(CH):
-            scan(ck("ED", c), ck(XS, c), ck(X, c), 0.0 if c == 0 else r("ED", 512 * c - 1, 512 * c), O.add, O.subtract)
+            scan(ck("ED", c), ck(XS, c), ck(XM, c), 0.0 if c == 0 else r("INY", c - 1, c), O.add, O.subtract)
             if QF[c] == "s":
                 act(ck("EA", c), ck("ED", c), F.Relu)
         for c in range(CH):
@@ -496,70 +519,78 @@ def rank_program(g, core, T, topo):
         op("v", lambda e: e.tensor_reduce(out=cn[0], in_=dm[0], axis=AxisListType.X, op=O.add), [cn], [dm])
 
     def count2():
-        cp(r("CI"), r("S0", 400, 401))
-        ts(r("CJ"), r("CI"), 31, O.bitwise_and)
-        tt(r("THC"), r("CJ"), r("TH"), O.add)
-        ts(r("SBI"), r("THC"), -1.0, O.mult, 0.5, O.add)
+        return [lambda: cp(r("CI"), r("S0", 400, 401)),
+                lambda: ts(r("CJ"), r("CI"), 31, O.bitwise_and),
+                lambda: tt(r("THC"), r("CJ"), r("TH"), O.add),
+                lambda: ts(r("SBI"), r("THC"), -1.0, O.mult, 0.5, O.add)]
 
     def ask1(t):
-        scan(r("M1"), r("KMX"), r("S1", 0, 144), 0.0, O.min, O.max)
-        tt(r("DD", 1, 144), r("S1", 1, 144), r("M1", 0, 143), O.min)
-        cp(r("K2S"), r("S1", 0, 144), "s")
+        errors(t)
+        h = []
         if t < 3:
-            claims(t + 1)
-        scan(r("M2"), r("KMX"), r("DD"), 0.0, O.min, O.max)
-        gather("v", r("OB"), r("M2"), r("L17"), r("K2S"), O.is_equal)
-        ts(r("ND"), r("M2"), 1.0, O.is_lt, r("DCOL"), O.mult)
-        tt(r("OBV"), r("OB"), r("VT"), O.mult)
-        scan(r("VB"), r("KMX"), r("OBV"), 0.0, O.min, O.max)
-        tt(r("OFS"), r("ND"), r("VB"), O.max)
+            names(t + 1)
+            h = hashes(t + 1)
+
+        def second():
+            tt(r("DD", 1, 144), r("S1", 1, 144), r("M1", 0, 143), O.min)
+            cp(r("K2S"), r("S1", 0, 144), "s")
+        scan(r("M1"), r("KMX"), r("S1", 0, 144), 0.0, O.min, O.max)
+        second()
+        run([lambda: scan(r("M2"), r("KMX"), r("DD"), 0.0, O.min, O.max),
+             lambda: gather("v", r("OB"), r("M2"), r("L17"), r("K2S"), O.is_equal),
+             lambda: tt(r("OBV"), r("OB"), r("R2", 0, 144), O.mult),
+             lambda: scan(r("VB"), r("KMX"), r("OBV"), 0.0, O.min, O.max),
+             lambda: tt(r("OFS"), r("ND"), r("VB"), O.max)],
+            [[lambda: gather("v", r("OA"), r("M1"), r("L17"), r("K2S"), O.is_equal),
+              lambda: ts(r("ND"), r("M2"), 1.0, O.is_lt, r("DCOL"), O.mult),
+              lambda: tt(r("OAV"), r("OA"), r("R2", 0, 144), O.mult),
+              lambda: scan(r("VA"), r("KMX"), r("OAV"), 0.0, O.min, O.max)], [lambda: None] * HS + h])
+        if t < 3:
+            claims(t + 1, 0, 2)
         gather("v", r("OFF"), r("OFS"), r("LC"))
         gather("v", r("OFM"), r("OFS"), r("LC"), r("MASKJ"), O.mult)
         mm(r("D0", 0, 128), r("OFF"), r("IDF"), True, True)
         mm(r("D0", 128, 136), r("OFM"), r("RSEL"), True, True)
-        gather("v", r("OA"), r("M1"), r("L17"), r("K2S"), O.is_equal)
-        tt(r("OAV"), r("OA"), r("VT"), O.mult)
-        scan(r("VA"), r("KMX"), r("OAV"), 0.0, O.min, O.max)
         gather("v", r("VAF"), r("VA"), r("LC"))
         mm(r("D1", 0, 128), r("VAF"), r("IDF"), True, True)
         if t < 3:
             act(r("DW"), r("D1", 0, 128), F.Identity, 0.0, r("C1"))
         cp(r("D32"), r("D1", 0, 128), "s")
+        if t < 3:
+            claims(t + 1, 2, 4)
+            shifted(t + 1)
 
     def ask2(t):
         for c in range(8):
             ts(r("EQ", 128 * c + 112 - 16 * c, 128 * c + 128), r("D0", 0, 16 * c + 16), r("D0", 128 + c, 129 + c), O.is_equal)
+        more = [lambda: ts(r("DR"), r("D1", 0, 128), MAG64, O.add, MAG64, O.subtract),
+                lambda: tt(r("DB"), r("DW"), r("DR"), O.subtract)]
+        run([lambda: scan(r("ST"), r("GRO"), r("EQ"), 0.0, O.mult, O.max),
+             lambda: ts(r("LO"), r("ST", 127, 1024, 128), r("THR"), O.is_ge),
+             lambda: tt(r("LO2"), r("LO"), r("DUM"), O.mult),
+             lambda: tt(r("OFL"), r("LO2"), r("D0", 128, 136), O.max),
+             lambda: cp(r("OFU"), r("OFL"))], [more + count2()[:3]] if t < 3 else [])
         if t < 3:
-            ts(r("DR"), r("D1", 0, 128), MAG64, O.add, MAG64, O.subtract)
-        scan(r("ST"), r("GRO"), r("EQ"), 0.0, O.mult, O.max)
-        if t < 3:
-            tt(r("DB"), r("DW"), r("DR"), O.subtract)
-        ts(r("LO"), r("ST", 127, 1024, 128), r("THR"), O.is_ge)
-        tt(r("LO2"), r("LO"), r("DUM"), O.mult)
-        tt(r("OFL"), r("LO2"), r("D0", 128, 136), O.max)
-        cp(r("OFU"), r("OFL"))
-        if t < 3:
+            count2()[3]()
             scatter(r("TB"), r("OFU"), r("DB"))
 
     start()
     names(0)
-    hashes(0)
+    run(hashes(0), [])
     claims(0)
     constants()
+    constants_b()
+    shifted(0)
     for t in range(4):
         main(t)
         landed("VU%d" % (t + 1), "rv%d" % (t + 1))
         landed("YH%d" % (t + 1), "ry%d" % (t + 1))
         if t < 3:
-            names(t + 1)
-            hashes(t + 1)
-            errors(t)
             ask1(t)
             ask2(t)
         else:
             cp(r("YVF"), r("VU4"))
             dma("y", inp(T.yv[:], "yv"), r("YVF"))
-            errors(t)
             ask1(t)
             ask2(t)
             scatter(r("T32"), r("OFU"), r("D32"))

from concourse.mybir import AluOpType as O, AxisListType, ActivationFunctionType as F

SCRATCH = {}
SEMAPHORES = ["qv", "qs", "qt", "qg", "ls"]
BF, F4, H2, I4, U2 = "bfloat16", "float32", "float16", "int32", "uint16"


def _b(name, cols, dtype="float32", where="sbuf"):
    SCRATCH[name] = (where, [128, cols], dtype)


for _n, _c, _d in [
        ("CL", 8192, BF), ("TB", 8320, BF), ("T32", 8320, F4),
        ("X0", 2048, BF), ("X1", 2048, BF), ("XS0", 2064, BF), ("XS1", 2064, BF), ("XM0", 2048, BF), ("XM1", 2048, BF),
        ("PG", 2048, BF), ("DZ", 2048, BF), ("AD", 2048, BF), ("SG", 2048, BF),
        ("SA", 2048, F4), ("SB", 2048, F4), ("FD", 2048, BF), ("FA", 2048, BF), ("ED", 2048, BF), ("EA", 2048, BF),
        ("VF0", 128, F4), ("VF1", 128, F4), ("S32", 128, F4), ("UI", 128, I4), ("UQ0", 128, I4), ("UQ1", 128, I4), ("HA", 128, F4), ("HB", 128, I4), ("HC", 128, I4), ("HX", 128, U2),
        ("S3P", 128, F4), ("PA", 128, F4), ("PB", 128, I4), ("PC", 128, I4), ("HZ", 128, U2),
        ("PV", 128, F4), ("DP", 128, F4), ("VN", 128, F4), ("DM", 128, BF), ("VT", 144, F4),
        ("SS", 128, F4), ("MH", 136, H2), ("YV", 136, BF), ("YS", 128, F4), ("YL", 8, U2),
        ("MN", 128, F4), ("MM", 128, F4), ("MR", 128, F4), ("K2S", 144, F4), ("M1", 144, F4), ("M2", 144, F4), ("DD", 144, F4),
        ("OB", 144, F4), ("OA", 144, F4), ("OBV", 144, F4), ("OAV", 144, F4), ("VB", 144, F4), ("VA", 144, F4),
        ("ND", 144, F4), ("OFS", 144, F4), ("OFF", 128, F4), ("OFM", 128, F4), ("VAF", 128, F4), ("D32", 128, F4), ("DR", 128, F4), ("DW", 128, F4), ("DB", 128, BF),
        ("L16", 8, U2), ("LC", 8, U2), ("L17", 9, U2), ("LI16", 8, F4), ("LIC", 9, F4), ("CI9", 9, F4), ("CG9", 9, F4), ("LS9", 9, F4), ("IDW", 144, F4),
        ("SR2", 8, BF), ("NY", 144, BF), ("NY1", 136, BF), ("EQ", 1024, BF), ("ST", 1024, BF), ("LO", 8, F4), ("LO2", 8, F4), ("OFL", 8, F4), ("OFU", 8, U2),
        ("CN", 1, F4), ("CI", 1, I4), ("CJ", 1, I4), ("THC", 1, F4), ("SBI", 1, F4), ("TH", 1, F4),
        ("ONB", 512, BF), ("ONF", 256, F4), ("IDB", 128, BF), ("IDP", 128, BF), ("IDN", 128, BF), ("IDP2", 128, BF), ("IDN2", 128, BF), ("X15", 128, F4), ("INI", 3, F4), ("INY", 3, F4), ("IDF", 128, F4),
        ("BK0", 128, BF), ("BLK", 128, BF), ("BL8", 8, BF), ("SR", 8, BF), ("DK", 2048, BF), ("EK", 2048, BF), ("WB", 128, H2), ("WC1", 1, F4), ("WC2", 1, F4), ("WCE", 1, F4), ("C1", 1, F4),
        ("PI4", 1, I4), ("PI5", 1, I4), ("PM", 1, F4), ("PM16", 1, F4), ("DCOL", 1, F4), ("THR", 1, F4), ("THB", 1, F4),
        ("PEN", 128, BF), ("KI", 136, F4), ("KC", 128, BF), ("KN", 136, F4), ("KN2", 136, F4), ("K2T", 136, F4), ("K2R", 144, F4), ("IW", 136, F4),
        ("JI", 128, F4), ("NK", 1, F4), ("NKH", 1, H2), ("MASKJ", 128, F4), ("RSEL", 8, F4), ("NRS", 8, F4), ("L0", 8, F4), ("LBASE", 8, F4), ("DU0", 8, F4), ("DUM", 8, F4),
        ("RMX", 512, BF), ("RMN", 512, BF), ("KMN", 128, F4), ("KMX", 144, F4), ("GRO", 1024, BF), ("SEL8", 128, F4),
        ("PAR", 512, I4), ("PF", 512, F4), ("P64", 512, F4), ("PH", 512, BF), ("PL", 512, BF),
        ("WI", 128, I4), ("E0", 128, BF), ("WT", 1, I4), ("WF", 1, F4), ("CW", 1, F4), ("LI", 2, I4), ("LF", 2, F4), ("N16", 1, F4),
        ("YVF", 128, F4), ("YEB", 128, BF)]:
    _b(_n, _c, _d)
for _t in range(5):
    for _n, _d in (("VU", U2), ("YH", H2), ("VO", U2), ("YO", H2)):
        _b("%s%d" % (_n, _t), 128, _d)
    SEMAPHORES += ["rv%d" % _t, "ry%d" % _t]
AL = {}
_pos = {}
for _n in list(SCRATCH):
    _w, _s, _d = SCRATCH[_n]
    if _s[1] <= 256 and _d in (BF, F4, I4):
        _p = _pos.get(_d, 0)
        AL[_n] = ("ALL_" + _d, _p, _s[1])
        _pos[_d] = _p + (_s[1] + 15) // 16 * 16
        del SCRATCH[_n]
for _d in _pos:
    _b("ALL_" + _d, _pos[_d], _d)
PSUM = ("R0", "R1", "R2", "R3", "D0", "D1", "S0", "S1")
for _n in PSUM:
    _b(_n, 512, F4, "psum")
SEMAPHORES += ["d%d" % i for i in range(20)]

NS = 8
CH = 4
QX = "ssss"
QP = "svsv"
QF = "ssvv"
HS = 1
MAG16, MAG64 = 1.5 * 2.0 ** 27, 1.5 * 2.0 ** 29


def rank_program(g, core, T, topo):
    rank = T.rank_of(core)
    if rank is None:
        return
    N = len(T.cores)
    eng = {"v": g.vector, "s": g.scalar, "t": g.tensor, "g": g, "y": g.sync}
    cnt = {"v": 0, "s": 0, "t": 0, "g": 0}
    tot, snap, hist, ndma = {}, {}, {}, [0]
    know = {q: {} for q in eng}

    def need(q, ins, outs):
        req = {}

        def add(e):
            if know[q].get(e[0], 0) < e[1]:
                req[e[0]] = max(req.get(e[0], 0), e[1])
        for (_, n, a, b) in ins:
            for (wa, wb, k, wq, e) in hist.get(n, ()):
                if n in PSUM:
                    if wq != q:
                        add(e)
                elif wa < b and a < wb and k == "w":
                    add(e)
        for (_, n, a, b) in outs:
            for (wa, wb, k, wq, e) in hist.get(n, ()):
                if n in PSUM:
                    if wq != q:
                        add(e)
                elif wa < b and a < wb and (wq != q or e[0][0] != "q" or k == "w"):
                    add(e)
        for s in list(req):
            for s2 in list(req):
                if s2 != s and s in req and s2 in req and snap[(s2, req[s2])].get(s, 0) >= req[s]:
                    del req[s]
        for s in sorted(req):
            eng[q].wait_ge(T.sem[s], req[s])
            for k2, v2 in snap[(s, req[s])].items():
                know[q][k2] = max(know[q].get(k2, 0), v2)
            know[q][s] = max(know[q].get(s, 0), req[s])

    def note(q, ins, outs, e):
        for (_, n, a, b) in outs:
            h = hist.setdefault(n, [])
            if n in PSUM:
                h[:] = [x for x in h if x[3] == q and x[4][1] > e[1]]
            else:
                h[:] = [x for x in h if not (a <= x[0] and x[1] <= b)]
            h.append((a, b, "w", q, e))
        for (_, n, a, b) in ins:
            h = hist.setdefault(n, [])
            h[:] = [x for x in h if not (x[2] == "r" and x[3] == q and x[4][0] == e[0] and a <= x[0] and x[1] <= b)]
            h.append((a, b, "r", q, e))

    def op(q, fn, outs, ins):
        need(q, ins, outs)
        s = "q" + q
        cnt[q] += 1
        snap[(s, cnt[q])] = dict(know[q])
        tot[s] = cnt[q]
        fn(eng[q]).then_inc(T.sem[s], 1)
        note(q, ins, outs, (s, cnt[q]))

    def dma(q, out, in_):
        need(q, [in_], [out])
        s = "d%d" % ndma[0]
        ndma[0] += 1
        snap[(s, 16)] = dict(know[q])
        tot[s] = 16
        eng[q].dma_start(out[0], in_[0]).then_inc(T.sem[s], 16)
        note(q, [in_], [out], (s, 16))

    def r(n, a=0, b=None, st=1, p=None):
        if n in AL:
            n, o, w = AL[n]
            b = min(o + (w if b is None else b), o + w)
            a = o + a
        b = T[n].shape[1] if b is None else b
        return (T[n][0:p, a:b:st] if p else T[n][:, a:b:st], n, a, b)

    def inp(ap, name):
        return (ap, name, 0, 1)

    def val(x):
        return x[0] if isinstance(x, tuple) else x

    def aps(*xs):
        return [x for x in xs if isinstance(x, tuple)]

    def tt(out, a, b, o):
        op("v", lambda e: e.tensor_tensor(out=out[0], in0=a[0], in1=b[0], op=o), [out], [a, b])

    def ts(out, a, s1, o1, s2=None, o2=None):
        if o2 is None:
            op("v", lambda e: e.tensor_scalar(out=out[0], in0=a[0], scalar1=val(s1), scalar2=None, op0=o1), [out], aps(a, s1))
        else:
            op("v", lambda e: e.tensor_scalar(out=out[0], in0=a[0], scalar1=val(s1), scalar2=val(s2), op0=o1, op1=o2), [out], aps(a, s1, s2))

    def cp(out, a, q="v"):
        if q == "v":
            op("v", lambda e: e.tensor_copy(out=out[0], in_=a[0]), [out], [a])
        else:
            op("s", lambda e: e.activation(out=out[0], in_=a[0], func=F.Copy), [out], [a])

    def act(out, a, f, bias=0.0, scale=1.0):
        op("s", lambda e: e.activation(out=out[0], in_=a[0], func=f, bias=val(bias), scale=val(scale)), [out], aps(a, bias, scale))

    def scan(out, d0, d1, init, o0, o1):
        op("v", lambda e: e.tensor_tensor_scan(out=out[0], data0=d0[0], data1=d1[0], initial=val(init), op0=o0, op1=o1), [out], aps(d0, d1, init))

    def ms(a, c):
        op("v", lambda e: e.memset(a[0], c), [a], [])

    def mm(out, l, rh, start, stop):
        op("t", lambda e: e.matmul(out[0], lhsT=l[0], rhs=rh[0], start=start, stop=stop), [out], [l, rh])

    def aff(out, a, pat, cmp, fill, base, chm):
        op("g", lambda e: e.affine_select(out=out[0], in_=a[0], pattern=pat, compare_op=cmp, fill=fill, base=base, channel_multiplier=chm), [out], [a])

    def iota(out, pat, base, chm):
        op("g", lambda e: e.iota(out[0], pattern=pat, base=base, channel_multiplier=chm, allow_small_or_imprecise_dtypes=True), [out], [])

    def gather(q, out, win, off, in1=None, o=None):
        ap = win[0].indirect(off[0])
        if in1 is not None:
            op("v", lambda e: e.tensor_tensor(out=out[0], in0=ap, in1=in1[0], op=o), [out], [win, off, in1])
        elif q == "v":
            op("v", lambda e: e.tensor_copy(out=out[0], in_=ap), [out], [win, off])
        else:
            op("s", lambda e: e.activation(out=out[0], in_=ap, func=F.Copy), [out], [win, off])

    def scatter(win, off, src):
        ap = win[0].indirect(off[0])
        op("v", lambda e: e.tensor_copy(out=ap, in_=src[0]), [win], [off, src])

    def send(to, src, dst, sem):
        c = T.cores[to % N]
        need("g", [src], [])
        m = sum(1 << e for e in topo.engines(core, c)[:NS])
        rid, pid, _ = topo.addr(c)
        g.remote_dma(out_ap=T[dst][:], in_ap=src[0], remote_sem=T.sem[sem], local_sem=T.sem.ls, pid=pid, routing_id=rid, dma_engine_mask=m)
        tot["ls"] = tot.get("ls", 0) + NS

    def landed(n, sem):
        tot[sem] = NS
        snap[(sem, NS)] = {}
        hist[n] = [(0, 128, "w", "far", (sem, NS))]

    def ck(n, c):
        return r(n, 512 * c, 512 * c + 512)

    def lk(n, c):
        return r(n, 32 * c, 32 * c + 32)

    def start():
        dma("s", r("PAR"), inp(T.par[:], "par"))
        dma("y", r("WI"), inp(T.who[:], "who"))
        dma("s", r("E0"), inp(T.est[:], "est"))
        dma("y", r("WT"), inp(T.wt[:], "wt"))
        dma("s", r("LI", 0, 2, 1, 8), inp(T.lim[:], "lim"))
        dma("y", r("CL"), inp(T.claim[:], "claim"))
        ms(r("ONB"), 1.0)
        ms(r("ONF"), 1.0)
        iota(r("PI4"), [[0, 1]], 0, 1)
        aff(r("BK0"), r("ONB", 0, 128), [[-16, 8], [0, 16]], O.is_ge, 0.0, 0, 1)
        aff(r("BLK"), r("BK0"), [[16, 8], [0, 16]], O.is_ge, 0.0, 15, -1)
        aff(r("SEL8", p=8), r("ONF", 0, 128, 1, 8), [[-1, 8], [0, 16]], O.is_equal, 0.0, 0, 1)
        aff(r("IDB"), r("ONB", 0, 128), [[-1, 128]], O.is_equal, 0.0, 0, 1)
        ms(r("NK"), -1024.0)
        ms(r("DK"), 0.0)
        cp(r("BL8"), r("BLK", 0, 128, 16))
        for k in range(16):
            cp(r("DK", 128 * k + k, 128 * k + 128, 16), r("BL8"), "s")
        ms(r("TB", 0, 5760), 0.0)
        for c in range(5):
            cp(r("TB", 5760 + 512 * c, 6272 + 512 * c), r("ONB"), "s")
        cp(r("PF"), r("PAR"))
        ts(r("P64"), r("PF"), MAG64, O.add, MAG64, O.subtract)
        act(r("PH"), r("P64"), F.Copy, 0.0, -1.0)
        tt(r("PL"), r("PF"), r("P64"), O.subtract)
        dma("y", (T.TB[1:128:16, 0:8192], "TB", 0, 8192), r("PH"))
        dma("s", (T.TB[2:128:16, 0:8192], "TB", 0, 8192), r("PL"))
        dma("y", (T.T32[0:128:16, 0:8192], "T32", 0, 8192), r("PF"))
        cp(r("VU0"), r("WI"))
        cp(r("WF"), r("WT"))
        ts(r("WB"), r("BLK"), r("WF"), O.mult)
        ts(r("YH0"), r("E0"), 1024.0, O.add)
        cp(r("NKH"), r("NK"))
        mm(r("S0", 496, 497), r("WB"), r("NKH"), True, True)
        cp(r("CW"), r("S0", 496, 497))
        ts(r("PI5"), r("PI4"), 15, O.bitwise_and)
        cp(r("PM"), r("PI5"))

    def constants():
        ts(r("WC1"), r("PM"), 1.0, O.is_equal)
        ts(r("WC2"), r("PM"), 2.0, O.is_equal)
        tt(r("WCE"), r("WC2"), r("WC1"), O.subtract)
        ts(r("EK"), r("DK"), r("WCE"), O.mult)
        cp(r("LF", 0, 2, 1, 8), r("LI", 0, 2, 1, 8))
        ts(r("N16", 0, 1, 1, 8), r("LF", 1, 2, 1, 8), -16.0, O.mult)
        mm(r("S0", 498, 499), r("SEL8", 0, 128, 1, 8), r("LF", 0, 1, 1, 8), True, True)
        cp(r("TH"), r("S0", 498, 499))
        cp(r("THC"), r("TH"))
        ts(r("SBI"), r("TH"), -1.0, O.mult, 0.5, O.add)
        ts(r("IDP"), r("IDB"), 128.0, O.mult)
        ts(r("IDN"), r("IDB"), -128.0, O.mult)
        ts(r("IDP2"), r("IDB"), 256.0, O.mult)
        ts(r("IDN2"), r("IDB"), -256.0, O.mult)
        ms(r("IDW"), 0.0)
        aff(r("IW"), r("ONF", 0, 136), [[-16, 8], [-1, 17]], O.is_equal, 0.0, 1, 1)
        aff(r("IDW", 0, 136), r("IW"), [[0, 8], [1, 17]], O.is_gt, 0.0, 0, 0)

    def constants_b():
        ms(r("RMX"), 1024.0)
        ms(r("RMX", 0, 512, 16), -1024.0)
        ms(r("RMN"), -1024.0)
        ms(r("RMN", 0, 512, 16), 1024.0)
        ts(r("MH", 0, 1), r("NK"), -1.0, O.mult)
        ms(r("YV", 0, 1), 0.0)
        iota(r("JI"), [[0, 8], [1, 16]], 0, 0)
        ts(r("KC"), r("JI"), -7.5, O.add)
        ts(r("PEN"), r("IDB"), 65536.0, O.mult)
        ts(r("SR"), r("BL8"), 16.0, O.mult)
        ts(r("SR2"), r("BL8"), 32.0, O.mult)
        ms(r("NY"), -16.0)
        aff(r("NY1"), r("NY", 0, 136), [[-16, 8], [0, 17]], O.is_ge, 0.0, 0, 1)
        aff(r("NY", 0, 136), r("NY1"), [[16, 8], [0, 17]], O.is_ge, 0.0, 15, -1)
        iota(r("KI"), [[0, 8], [1, 17]], 0, 0)
        iota(r("LI16"), [[16, 8]], 15, 0)
        iota(r("L0"), [[256, 8]], 0, 0)
        iota(r("LIC"), [[17, 9]], 16, 0)
        iota(r("CI9"), [[1, 9]], 0, 0)
        iota(r("DCOL"), [[0, 1]], 8192, 1)
        iota(r("DU0"), [[16, 8]], 8192, 0)
        ms(r("KMX"), 8388608.0)
        ms(r("DD"), -8388608.0)
        ms(r("KMX", 0, 144, 17), -8388608.0)
        ms(r("GRO"), 1.5)
        ms(r("EQ"), 0.0)
        ms(r("GRO", 0, 1024, 128), 0.0)
        ts(r("KN"), r("KI"), -1.0, O.mult, 17.0, O.add)
        aff(r("KN2"), r("KN"), [[0, 8], [1, 17]], O.is_gt, -4194304.0, 0, 0)

    def constants_c():
        ts(r("MASKJ"), r("JI"), r("PM"), O.is_equal)
        cp(r("IDF"), r("IDB"))
        cp(r("RSEL"), r("BL8"))
        ts(r("NRS"), r("RSEL"), -1.0, O.mult)
        ts(r("PM16"), r("PM"), 16.0, O.mult)
        cp(r("L16"), r("LI16"))
        ts(r("LBASE"), r("L0"), r("PM16"), O.add, 7.5, O.add)
        ms(r("KMN"), -8388608.0)
        ms(r("KMN", 0, 128, 16), 8388608.0)
        ts(r("K2T", 0, 136, 1, 8), r("KN2", 0, 136, 1, 8), r("N16", 0, 1, 1, 8), O.add)
        ms(r("K2R"), 0.0)
        aff(r("K2R", 0, 136, 1, 8), r("K2T", 0, 136, 1, 8), [[-1, 8], [0, 17]], O.is_equal, 0.0, 0, 1)

    def constants_d():
        ts(r("C1"), r("PM"), 1.0, O.not_equal)
        cp(r("LC"), r("LIC", 0, 8))
        ts(r("CG9"), r("CI9"), r("PM"), O.is_gt, -17.0, O.mult)
        tt(r("LS9"), r("LIC"), r("CG9"), O.add)
        ts(r("L17"), r("LS9"), 143.0, O.min)
        ts(r("DUM"), r("DU0"), r("PM"), O.add)
        ms(r("THB"), 6.3051201)
        act(r("THR"), r("PM"), F.Exp, r("THB"), -0.4054651)

    def run(steps, others):
        others = [list(o) for o in others]
        for f in steps:
            f()
            for o in others:
                if o:
                    o.pop(0)()
        for o in others:
            for f in o:
                f()

    def names(t):
        cp(r("VF%d" % (t & 1)), r("VU%d" % t))
        act(r("S32"), r("VF%d" % (t & 1)), F.Copy, 32.0 * 77 * t - 262144.0, 32.0)

    def hashes(t):
        UQ = "UQ%d" % (t & 1)
        mm(r("S0", 0, 128), r("WB"), r("YH%d" % t), True, True)
        return [lambda: ts(r("UI"), r("S0", 0, 128), r("CW"), O.add),
                lambda: ts(r(UQ), r("UI"), 2047, O.bitwise_and),
                lambda: tt(r("HA"), r("VF%d" % (t & 1)), r(UQ), O.mult),
                lambda: tt(r("HB"), r("HA"), r("S32"), O.add),
                lambda: ts(r("HC"), r("HB"), 5, O.arith_shift_right, 8191, O.bitwise_and),
                lambda: cp(r("HX"), r("HC"))]

    def claims(t, a=0, b=CH):
        for c in range(a, b):
            gather(QX[c], ck("X%d" % (t & 1), c), r("CL"), lk("HX", c))

    def shifted(t):
        X, XS, XM = "X%d" % (t & 1), "XS%d" % (t & 1), "XM%d" % (t & 1)
        for c in range(CH):
            aff(ck(XM, c), ck(X, c), [[0, 512]], O.is_gt, 0.0, 1, 0)
        for c in range(CH):
            aff(r(XS, 512 * c + 1, 512 * c + 513), ck(X, c), [[0, 512]], O.is_gt, 0.0, 1, 0)

    def main(t):
        p = t & 1
        X, XS, XM, VF, UQ = "X%d" % p, "XS%d" % p, "XM%d" % p, "VF%d" % p, "UQ%d" % p
        R, R2 = ["R0", "R1", "R2", "R3"], ["D0", "D1", "R0", "R1"]
        to = rank + (3 if t < 3 else -9)
        for c in range(CH):
            gather(QP[c] if t else "s", ck("PG", c), r("TB", 0, 8192), lk("VU%d" % t, c))

        def masked(c):
            mm(r(R[c]), r("IDP" if c < 3 else "IDP2"), ck("SG", c), False, True)

        def turned(c):
            mm(r(R2[c]), r("IDN" if c < 3 else "IDN2"), ck("SG", c), False, True)

        def plain(c):
            mm(r(R2[c]), r("IDB"), ck(X, c), True, False)

        for c in range(CH):
            mm(r(R[c]), r("IDB"), ck(X, c), True, False)
        PP = [r("S0", 128, 192), r("S1", 288, 352)]
        for h in range(2):
            for k in range(16):
                mm(PP[h], r("EK", 128 * k, 128 * k + 128), r("PG", 1024 * h + k, 1024 * h + 1024, 16), k == 0, k == 15)

        def hashp(h):
            a, b = 64 * h, 64 * h + 64
            return [lambda: tt(r("PA", a, b), PP[h], r(UQ, a, b), O.mult),
                    lambda: tt(r("PB", a, b), r("PA", a, b), r("S3P", a, b), O.add),
                    lambda: ts(r("PC", a, b), r("PB", a, b), 5, O.arith_shift_right, 8191, O.bitwise_and),
                    lambda: cp(r("HZ", a, b), r("PC", a, b))]

        def change(h):
            tt(r("PV", 64 * h, 64 * h + 64), PP[h], r(VF, 64 * h, 64 * h + 64), O.subtract)

        def dist(c):
            gather("v", ck("DZ", c), r("CL"), lk("HZ", c), ck(X, c), O.subtract)
            act(ck("AD", c), ck("DZ", c), F.Abs)

        def total(c):
            mm(r("D%d" % (c & 1)), r("BLK"), ck("AD", c), True, True)

        def sign(c):
            act(ck("SG", c), r("D%d" % (c & 1)), F.Sign, r("SBI"))

        for h in range(2):
            act(r("S3P", 64 * h, 64 * h + 64), PP[h], F.Copy, 32.0 * 77 * t - 262144.0, 32.0)
        run(hashp(0), [])
        first, second = hashp(1)[:2], hashp(1)[2:]
        first[0]()
        dist(0)
        total(0)
        first[1]()
        dist(1)
        total(1)
        second[0]()
        change(0)
        change(1)
        second[1]()
        sign(0)
        dist(2)
        masked(0)
        total(2)
        sign(1)
        dist(3)
        masked(1)
        total(3)
        if t == 0:
            constants_c()
        else:
            scatter(r("T32"), r("OFU"), r("D32"))
        sign(2)
        masked(2)
        plain(0)
        turned(0)
        ts(r("X15"), r(X, 15, 2048, 16), 1024.0, O.add)
        tt(r(XM, 16, 2048, 16), r(X, 16, 2048, 16), r(X, 15, 2047, 16), O.subtract)
        for c in range(CH):
            scan(ck("SA", c), r("RMX"), r(R[c]), 0.0, O.min, O.max)
            if c == 1:
                ts(ck("SG", 3), r("D1"), r("THC"), O.is_ge)
                masked(3)
                plain(2)
                turned(2)
                plain(1)
                turned(1)
                plain(3)
                turned(3)
        mm(r("R2", 0, 144), r(VF), r("IDW"), True, True)
        for k in range(16):
            mm(r("R3", 0, 128), r("DK", 128 * k, 128 * k + 128), r("AD", k, 2048, 16), k == 0, k == 15)
        for c in (0, 2, 1, 3):
            scan(ck("SB", c), r("RMN"), r(R2[c]), 0.0, O.max, O.min)
        run([lambda: tt(r("SS"), r("SA", 15, 2048, 16), r("SB", 15, 2048, 16), O.add),
             lambda: ts(r("MH", 1, 129), r("SS"), 0.5, O.mult, 1023.8, O.add),
             lambda: tt(r(XS, 0, 2048, 16), r("MH", 1, 129), r("MH", 0, 128), O.subtract)],
            [[lambda: ts(r("DM"), r("R3", 0, 128), r("THC"), O.is_lt),
              lambda: tt(r("DP"), r("PV"), r("DM"), O.mult),
              lambda: tt(r("VN"), r("DP"), r(VF), O.add)]])
        tt(r("INI"), r("MH", 32, 128, 32), r("X15", 31, 127, 32), O.subtract)
        cp(r("VO%d" % t), r("VN"))
        send(to, r("VO%d" % t), "VU%d" % (t + 1), "rv%d" % (t + 1))
        for c in range(CH):
            scan(ck("FD", c), ck(XS, c), ck(XM, c), 0.0 if c == 0 else r("INI", c - 1, c), O.add, O.subtract)
            if QF[c] == "s":
                act(ck("FA", c), ck("FD", c), F.Relu)
        for c in range(CH):
            if QF[c] == "v":
                ts(ck("FA", c), ck("FD", c), 0.0, O.max)
        mm(r("S1", 0, 128), r("ONB", 0, 128, 1, 1), r("KC", 0, 128, 1, 1), True, False)
        for k in range(16):
            mm(r("S1", k, 128, 16), r(X, k, 2048, 16), r("SR"), False, False)
        mm(r("S0", 256, 264), r("IDF"), r("LBASE"), True, False)
        mm(r("S1", 0, 128), r("DM"), r("PEN"), False, False)
        for k in range(16):
            mm(r("S1", k, 128, 16), r("FA", k, 2048, 16), r("SR2"), False, k == 15)
        scan(r("MN"), r("KMN"), r("S1", 0, 128), 0.0, O.max, O.min)
        gather("v", r("MM"), r("MN"), r("L16"), r("MASKJ"), O.mult)
        mm(r("S0", 256, 264), r("MM"), r("RSEL"), False, False)
        ts(r("MR"), r("MM"), MAG16, O.add, MAG16, O.subtract)
        mm(r("S0", 256, 264), r("MR"), r("NRS"), False, True)
        if t < 3:
            count1()
        cp(r("YL"), r("S0", 256, 264))
        if t < 3:
            mm(r("S0", 400, 401), r("ONF", 0, 128), r("CN"), True, True)
        gather("v", r("YS"), r(X), r("YL"), r("YH%d" % t), O.add)
        gather("v", r("YV", 1, 129), r(X), r("YL"))
        ts(r("YO%d" % t), r("YS"), 0.5, O.mult, 511.8, O.add)
        send(to, r("YO%d" % t), "YH%d" % (t + 1), "ry%d" % (t + 1))
        tt(r(XS, 0, 2048, 16), r("YV", 1, 129), r("YV", 0, 128), O.subtract)
        tt(r("INY"), r("YV", 32, 128, 32), r(X, 511, 2047, 512), O.subtract)
        mm(r("S1", 0, 144), r("ONF", 0, 128, 1, 8), r("K2R", 0, 144, 1, 8), True, False)
        for k in range(16):
            mm(r("S1", 1 + k, 136, 17), r(X, k, 2048, 16), r("SR"), False, False)
        mm(r("S1", 0, 144), r("YV", 1, 129), r("NY"), False, False)
        for c in range(CH):
            scan(ck("ED", c), ck(XS, c), ck(XM, c), 0.0 if c == 0 else r("INY", c - 1, c), O.add, O.subtract)
            if QF[c] == "s":
                act(ck("EA", c), ck("ED", c), F.Relu)
        for c in range(CH):
            if QF[c] == "v":
                ts(ck("EA", c), ck("ED", c), 0.0, O.max)
        if t == 0:
            constants_d()

    def errors(t):
        for k in range(16):
            mm(r("S1", 1 + k, 136, 17), r("EA", k, 2048, 16), r("SR2"), False, k == 15)

    def count1():
        cn, dm = r("CN"), r("DM")
        op("v", lambda e: e.tensor_reduce(out=cn[0], in_=dm[0], axis=AxisListType.X, op=O.add), [cn], [dm])

    def count2():
        return [lambda: cp(r("CI"), r("S0", 400, 401)),
                lambda: ts(r("CJ"), r("CI"), 31, O.bitwise_and),
                lambda: tt(r("THC"), r("CJ"), r("TH"), O.add),
                lambda: ts(r("SBI"), r("THC"), -1.0, O.mult, 0.5, O.add)]

    def ask1(t):
        errors(t)
        h = []
        if t < 3:
            names(t + 1)
            h = hashes(t + 1)

        def second():
            tt(r("DD", 1, 144), r("S1", 1, 144), r("M1", 0, 143), O.min)
            cp(r("K2S"), r("S1", 0, 144), "s")
        scan(r("M1"), r("KMX"), r("S1", 0, 144), 0.0, O.min, O.max)
        second()
        run([lambda: scan(r("M2"), r("KMX"), r("DD"), 0.0, O.min, O.max),
             lambda: gather("v", r("OB"), r("M2"), r("L17"), r("K2S"), O.is_equal),
             lambda: tt(r("OBV"), r("OB"), r("R2", 0, 144), O.mult),
             lambda: scan(r("VB"), r("KMX"), r("OBV"), 0.0, O.min, O.max),
             lambda: tt(r("OFS"), r("ND"), r("VB"), O.max)],
            [[lambda: gather("v", r("OA"), r("M1"), r("L17"), r("K2S"), O.is_equal),
              lambda: ts(r("ND"), r("M2"), 1.0, O.is_lt, r("DCOL"), O.mult),
              lambda: tt(r("OAV"), r("OA"), r("R2", 0, 144), O.mult),
              lambda: scan(r("VA"), r("KMX"), r("OAV"), 0.0, O.min, O.max)], [lambda: None] * HS + h])
        if t < 3:
            claims(t + 1, 0, 2)
        gather("v", r("OFF"), r("OFS"), r("LC"))
        gather("v", r("OFM"), r("OFS"), r("LC"), r("MASKJ"), O.mult)
        mm(r("D0", 0, 128), r("OFF"), r("IDF"), True, True)
        mm(r("D0", 128, 136), r("OFM"), r("RSEL"), True, True)
        gather("v", r("VAF"), r("VA"), r("LC"))
        mm(r("D1", 0, 128), r("VAF"), r("IDF"), True, True)
        if t < 3:
            act(r("DW"), r("D1", 0, 128), F.Identity, 0.0, r("C1"))
        cp(r("D32"), r("D1", 0, 128), "s")
        if t < 3:
            claims(t + 1, 2, 4)
            shifted(t + 1)

    def ask2(t):
        for c in range(8):
            ts(r("EQ", 128 * c + 112 - 16 * c, 128 * c + 128), r("D0", 0, 16 * c + 16), r("D0", 128 + c, 129 + c), O.is_equal)
        more = [lambda: ts(r("DR"), r("D1", 0, 128), MAG64, O.add, MAG64, O.subtract),
                lambda: tt(r("DB"), r("DW"), r("DR"), O.subtract)]
        run([lambda: scan(r("ST"), r("GRO"), r("EQ"), 0.0, O.mult, O.max),
             lambda: ts(r("LO"), r("ST", 127, 1024, 128), r("THR"), O.is_ge),
             lambda: tt(r("LO2"), r("LO"), r("DUM"), O.mult),
             lambda: tt(r("OFL"), r("LO2"), r("D0", 128, 136), O.max),
             lambda: cp(r("OFU"), r("OFL"))], [more + count2()[:3]] if t < 3 else [])
        if t < 3:
            count2()[3]()
            scatter(r("TB"), r("OFU"), r("DB"))

    start()
    names(0)
    run(hashes(0), [])
    claims(0)
    constants()
    constants_b()
    shifted(0)
    for t in range(4):
        main(t)
        landed("VU%d" % (t + 1), "rv%d" % (t + 1))
        landed("YH%d" % (t + 1), "ry%d" % (t + 1))
        if t < 3:
            ask1(t)
            ask2(t)
        else:
            cp(r("YVF"), r("VU4"))
            dma("y", inp(T.yv[:], "yv"), r("YVF"))
            ask1(t)
            ask2(t)
            scatter(r("T32"), r("OFU"), r("D32"))
            dma("y", inp(T.yp[:], "yp"), (T.T32[0:128:16, 0:8192], "T32", 0, 8192))
            ts(r("YEB"), r("YH4"), -1024.0, O.add)
            dma("s", inp(T.ye[:], "ye"), r("YEB"))
    for s in sorted(tot):
        g.wait_ge(T.sem[s], tot[s])
